import numpy as np, ml_dtypes
CORES = [3,11,19,27,35,43,51,59]
N = 8
import mx_ref
BF = ml_dtypes.bfloat16
def pick(q, e):
    c = np.concatenate([q[0].reshape(128, -1, 4), np.zeros((128, 1, 4), np.uint8)], axis=1); s = np.concatenate([q[1], np.ones((16, 1), np.uint8)], axis=1)
    return (np.ascontiguousarray(c[:, e].reshape(128, -1)), np.ascontiguousarray(s[:, e]))
def join(*qs):
    return (np.concatenate([q[0] for q in qs], axis=1), np.concatenate([q[1] for q in qs], axis=1))
def put(q, e, v):
    c, s = q[0].reshape(128, -1, 4).copy(), q[1].copy(); c[:, e] = v[0].reshape(128, -1, 4); s[:, e] = v[1]
    return (c.reshape(128, -1), s)
def pk(c, s):
    return (np.ascontiguousarray(c), mx_ref.live(s))
def emit(q):
    return q[0], q[1]
def decode(q):
    o = []
    for b in range(4):
        e = np.zeros((128, 128, 4), np.float32); e[np.arange(128), np.arange(128), b] = 1
        o.append(mx_ref.matmul(mx_ref.quantize(e.reshape(128, 512).astype(BF)), q))
    return np.stack(o, axis=2).reshape(128, -1)
def cols(t, e):
    v = np.concatenate([t.reshape(128, -1, 4), np.zeros((128, 1, 4), BF)], axis=1)
    return np.ascontiguousarray(v[:, e]).reshape(128, -1)
def cut(t, i, w=512):
    return t[:, w * i:w * i + w]
def f(rng, *shape):
    return mx_ref.flush((rng.standard_normal(shape, dtype=np.float32) * np.exp2(rng.integers(-2, 3, shape[:-1] + (1,)))).astype(BF))
def wide(rng, *shape, cols=0):
    v = rng.standard_normal(shape, dtype=np.float32) * np.exp2(rng.integers(-12, 13, shape)).astype(np.float32)
    if cols: v *= np.repeat(np.exp2(rng.integers(-cols, cols + 1, shape[:-2] + (1, shape[-1] // 4))) * (rng.random(shape[:-2] + (1, shape[-1] // 4)) > 0.0625), 4, axis=-1).astype(np.float32)
    return mx_ref.flush(v.astype(BF))
C, T, R, O = 256, 64, 3, 1
def trim(v):
    v = v.astype(np.float32)
    v[np.abs(v) < np.float32(2.0 ** -14)] = 0
    return v.astype(BF)
def given(rng, u, x):
    return {"kb": np.stack([trim(u.reshape(128, 4 * C))] * N), "x": trim(x.reshape(N, 128, 4 * R * T)), "w": f(rng, N, 128, 512 * O)}
def sturdy(rng, n):
    return (1 + rng.random((128, n, 4))) * rng.choice([-1.0, 1.0], (128, n, 4)) * np.exp2(rng.integers(-1, 2, (128, 1, 1)))
def kept(v):
    m, e = np.frexp(v)
    return np.ldexp(np.trunc(m * 8) * 0.125, e)
def near(rng, u, e):
    return u[:, e] + 0.5 * sturdy(rng, len(e))
def setup_inputs(rng):
    return given(rng, f(rng, 128, 4 * C), f(rng, N, 128, 4 * R * T))
def setup_inputs_both(rng):
    u, x, new = kept(sturdy(rng, C)), np.zeros((N, 128, R, T, 4)), np.zeros((N, C), bool)
    for b in range(R):
        for j, r in enumerate(rng.permutation([v for v in range(N) if v < v ^ (1 << b)])):
            p, e = r ^ (1 << b), rng.permutation(C)
            if j % 2: e = e[np.argsort(new[r, e] | ~new[p, e], kind="stable")]
            t = e[T:2 * T] if j % 2 else rng.permutation(e[:T])
            x[r, :, b] = near(rng, u, e[:T])
            x[r, :, b, :T // 4] = u[:, e[:T // 4]]
            x[p, :, b] = near(rng, u, t)
            for s in (r, p):
                new[s, e[:T]] = True
                new[s, t] = True
    return given(rng, u, x)
def setup_inputs_few(rng):
    u, x, four = sturdy(rng, C), np.zeros((N, 128, R, T, 4)), rng.permutation(C)[:4]
    for b in range(R):
        for j, r in enumerate(rng.permutation([v for v in range(N) if v < v ^ (1 << b)])):
            a = rng.permutation(four)[:2]
            for s, c in ((r, a[0]), (r ^ (1 << b), a[j % 2])):
                x[s, :, b] = near(rng, u, np.full(T, c)) * np.exp2(rng.integers(-1, 2, (1, T, 1)))
    return given(rng, u, x)
def setup_inputs_ties(rng):
    u = np.abs(cols(f(rng, 128, 4 * (C // 4)), rng.permutation(np.arange(C) % (C // 4))).astype(np.float32))
    x = np.abs(f(rng, N, 128, 4 * R * T).astype(np.float32)).reshape(N, 128, R, T, 4)
    for r in range(N):
        for b in range(R):
            x[r, :, b] *= (1 - 2 * (rng.permutation(T) % 2)).astype(np.float32)[:, None]
            x[r, :, b, int(rng.integers(0, T))] = 0
    return given(rng, u * np.float32(2.0 ** 18), x * np.float32(2.0 ** 18))
def setup_inputs_drift(rng):
    top = (rng.permutation(128) < 64)[:, None, None]
    u, z, x = sturdy(rng, C) * top, sturdy(rng, 8) * ~top, np.zeros((N, 128, R, T, 4))
    e = rng.permutation(C)
    for r in range(N):
        for b in range(R):
            t = rng.permutation(e[:C // 2] if b == 0 else e[C // 2:])[:T]
            x[r, :, b] = near(rng, u, t) * top + 8 * z[:, rng.permutation(np.arange(T) % 8)]
    return given(rng, u, x)
def setup_inputs_spread(rng):
    d = given(rng, wide(rng, 128, 4 * C, cols=2), wide(rng, N, 128, 4 * R * T, cols=6))
    d["kb"][:, :, :4] = BF(-0.0)
    for r in range(N):
        for b in range(R):
            i = 4 * (b * T + int(rng.integers(0, T)))
            d["x"][r, :, i:i + 4] = BF(0.0)
    return d
def check_inputs(d):
    b = []
    for n, lo, hi in (("kb", -14, 24), ("x", -14, 24), ("w", -30, 30)):
        v = np.abs(d[n].astype(np.float32))
        if not (np.isfinite(v).all() and ((v == 0) | (v >= 2.0 ** lo) & (v <= 2.0 ** hi)).all()): b.append("a value of " + n)
    if (d["kb"].astype(np.float32) != d["kb"][:1].astype(np.float32)).any(): b.append("kb isn't the same on all ranks")
    return b
def numbers(k, e):
    return decode(pick(k, np.concatenate([e, np.full(-len(e) % 4, -1)]))).reshape(128, -1, 4)[:, :len(e)]
def anew(k, e, v):
    t = np.zeros((128, len(e) + -len(e) % 4, 4), np.float32)
    t[:, :len(e)] = v
    return put(k, e, pick(mx_ref.quantize(t.reshape(128, -1).astype(BF)), np.arange(len(e))))
def reference(kb, x, w):
    k = join(*[mx_ref.quantize(np.ascontiguousarray(kb[r])) for r in range(N)])
    q = join(*[mx_ref.quantize(np.ascontiguousarray(x[r])) for r in range(N)])
    dx = decode(q).reshape(128, N, R, T, 4)
    ch = np.zeros((N, R, T), np.float32)
    for b in range(R):
        won, e, t = np.zeros((N, C), bool), [], []
        for r in range(N):
            v = pick(q, (r * R + b) * T + np.arange(T))
            s = np.concatenate([mx_ref.matmul(pick(k, C * r + 128 * m + np.arange(128)), v) for m in range(C // 128)])
            win = np.argmax(s + np.float32(0), axis=0)
            u, i = np.unique(win, return_index=True)
            won[r, u] = True
            e.append(C * r + u)
            t.append(dx[:, r, b, i])
            ch[r, b] = win
        e = np.concatenate(e)
        k = anew(k, e, np.float32(0.75) * numbers(k, e) + np.float32(0.25) * np.concatenate(t, axis=1))
        src, low, high = np.arange(N * C).reshape(N, C), [], []
        for r in range(N):
            p = r ^ (1 << b)
            src[r] = np.where(won[p] & ~won[r], C * p + np.arange(C), src[r])
            if r < p:
                u = np.flatnonzero(won[r] & won[p])
                low.append(C * r + u)
                high.append(C * p + u)
        low, high = np.concatenate(low), np.concatenate(high)
        if len(low):
            v = np.float32(0.5) * numbers(k, low) + np.float32(0.5) * numbers(k, high)
            k = anew(k, np.concatenate([low, high]), np.concatenate([v, v], axis=1))
        k = pick(k, src.reshape(-1))
    oc, osc, y = np.zeros((N, 128, 4 * C), np.uint8), np.zeros((N, 16, C), np.uint8), np.zeros((N, 128, O * C), np.float32)
    for r in range(N):
        t = pick(k, C * r + np.arange(C))
        oc[r], osc[r] = emit(t)
        for o in range(O): y[r, :, C * o:C * o + C] = mx_ref.matmul(mx_ref.quantize(np.ascontiguousarray(cut(w[r], o))), t)
    return {"oc": oc, "osc": osc, "ch": ch, "y": y}

@@ -1,0 +1,266 @@
+from concourse.mybir import dt, AluOpType, ActivationFunctionType
+
+ALU = AluOpType
+ACTF = ActivationFunctionType
+R = 3
+NT = 64
+
+X4 = "float8_e4m3fn_x4"
+SCRATCH = {"ps": ("psum", [128, 2048], "float32"), "pd": ("psum", [128, 2048], "float32"),
+           "pidx": ("sbuf", [128, 1], "int32"), "pand": ("sbuf", [128, 1], "int32")}
+for _n, _w in (("xt", 1024), ("kt", 1024), ("wt", 512), ("ones", 516), ("z1", 516), ("z3", 516), ("hs", 512), ("hm", 512),
+               ("hz", 512), ("sg0", 256), ("sg1", 256), ("sg2", 256), ("sg3", 256)):
+    SCRATCH[_n] = ("sbuf", [128, _w], "bfloat16")
+for _n, _w in (("qc", 1), ("qm", 1), ("repi", 32), ("c16", 320), ("row", 384), ("iq", 260), ("mk", 260), ("diag", 320),
+               ("rs", 256), ("base", 320), ("neg", 256), ("pm0", 256), ("pm1", 256), ("pm2", 256), ("pm3", 256),
+               ("eqb", 260), ("eqa", 260), ("dsb", 260), ("dsa", 260), ("ra", 64), ("g1", 64), ("s1", 64), ("t2", 64),
+               ("t3", 64), ("va", 64), ("ls", 256), ("yt", 256)):
+    SCRATCH[_n] = ("sbuf", [128, _w], "float32")
+for _n, _w in (("e1", 512), ("e3", 512), ("xq", 256), ("wq", 128), ("k3", 256)):
+    SCRATCH[_n] = ("sbuf", [128, _w], X4)
+    SCRATCH[_n + "s"] = ("sbuf", [128, _w], "uint8")
+for _b in range(R):
+    for _n, _w in (("win", 640), ("pj", 128), ("tr", 512)):
+        SCRATCH["%s%d" % (_n, _b)] = ("sbuf", [128, _w], X4)
+        SCRATCH["%ss%d" % (_n, _b)] = ("sbuf", [128, _w], "uint8")
+    for _n, _w in (("rep", 32), ("wb", 4), ("wa", 4), ("ub", 4), ("ua", 4), ("jl", 4), ("ll", 16)):
+        SCRATCH["%s%d" % (_n, _b)] = ("sbuf", [128, _w], "uint16")
+    for _n, _w in (("mi", 320), ("mc", 320), ("ml", 320), ("rb", 64)):
+        SCRATCH["%s%d" % (_n, _b)] = ("sbuf", [128, _w], "float32")
+
+SEMAPHORES = ["cv", "ca", "cp", "cg", "lx0", "lx1", "lk", "lw", "st", "loc"]
+for _b in range(R):
+    SEMAPHORES += ["rl%d" % _b, "rd%d" % _b]
+
+
+def rank_program(g, core, T, topo):
+    rank = T.rank_of(core)
+    if rank is None:
+        return
+    queues = {"V": (g.vector, "cv"), "A": (g.scalar, "ca"), "P": (g.tensor, "cp"), "G": (g, "cg"), "S": (g.sync, None)}
+    issued = {"cv": 0, "ca": 0, "cp": 0, "cg": 0}
+    known = {q: {} for q in queues}
+
+    def need(q, deps):
+        for sem, val, through in deps:
+            if known[q].get(sem, 0) < val:
+                queues[q][0].wait_ge(T.sem[sem], val)
+                known[q][sem] = val
+                for s, v in through.items():
+                    known[q][s] = max(known[q].get(s, 0), v)
+
+    def do(q, deps, fn, *args, **kw):
+        need(q, deps)
+        sem = queues[q][1]
+        issued[sem] += 1
+        fn(*args, **kw).then_inc(T.sem[sem], 1)
+        return (sem, issued[sem], dict(known[q]))
+
+    def dma(q, deps, sem, out, in_):
+        need(q, deps)
+        queues[q][0].dma_start(out, in_).then_inc(T.sem[sem], 16)
+        return (sem, 16, dict(known[q]))
+
+    vec, act, ten = g.vector, g.scalar, g.tensor
+
+    def V(deps, fn, *args, **kw):
+        return do("V", deps, fn, *args, **kw)
+
+    def A(deps, fn, *args, **kw):
+        return do("A", deps, fn, *args, **kw)
+
+    def mx(deps, bank, st, a, mv, c, n, start, stop):
+        return do("P", deps, ten.matmul_mx, bank, T[st[0]][:, a:a + 128], T[st[1]][:, a:a + 128],
+                  T[mv[0]][:, c:c + n], T[mv[1]][:, c:c + n], start, stop)
+
+    def w8(name, a, b):
+        return T[name][:, a:b].bitcast(dt.uint8)
+
+    def w32(name, a, b):
+        return T[name][:, a:b].bitcast(dt.uint32)
+
+    def pick(out, a, b, win, c, d, off, deps):
+        tc = V(deps, vec.tensor_copy, w32(out[0], a, b), w32(win[0], c, d).indirect(off))
+        ts = A(deps, act.activation, T[out[1]][:, a:b], T[win[1]][:, c:d].indirect(off), ACTF.Copy)
+        return [tc, ts]
+
+    lx0 = dma("S", [], "lx0", T.xt[:, 0:512], T.x[:, 0:512])
+    lk = dma("A", [], "lk", T.kt[:], T.kb[:])
+    lx1 = dma("S", [], "lx1", T.xt[:, 512:768], T.x[:, 512:768])
+
+    t_ones = V([], vec.memset, T.ones[:], 1.0)
+    t_pidx = do("G", [], g.iota, T.pidx[:], [[0, 1]], 0, 1)
+    t_repi = do("G", [], g.iota, T.repi[:], [[16, 4], [0, 8]], 0, 0, allow_small_or_imprecise_dtypes=True)
+    t_z1 = do("G", [t_ones], g.affine_select, T.z1[:], T.ones[:], [[-1, 516]], ALU.is_equal, 0.0, 3, 4)
+    t_c16 = do("G", [], g.iota, T.c16[:], [[0, 20], [1, 16]], 0, 0, allow_small_or_imprecise_dtypes=True)
+    t_row = do("G", [], g.iota, T.row[:], [[1, 384]], 0, 0, allow_small_or_imprecise_dtypes=True)
+    t_iq = do("G", [], g.iota, T.iq[:], [[-16, 4], [1, 65]], 0, 0, allow_small_or_imprecise_dtypes=True)
+
+    t_and = V([t_pidx], vec.tensor_scalar, T.pand[:], T.pidx[:], 15, None, ALU.bitwise_and)
+    t_hz = V([], vec.memset, T.hz[:], 0.0)
+    t_q = V([t_and], vec.tensor_copy, T.qc[:], T.pand[:])
+    t_xz = V([], vec.memset, T.xt[:, 768:1024], 0.0)
+    t_rep = [V([t_q, t_repi], vec.tensor_scalar, T["rep%d" % b][:], T.repi[:], T.qc[:], float(NT * b), ALU.add, ALU.add)
+             for b in range(R)]
+    t_hs = V([], vec.memset, T.hs[:], 0.0)
+    t_hm = V([], vec.memset, T.hm[:], 0.0)
+    t_neg = V([], vec.memset, T.neg[:], -1.0e29)
+    t_qm = V([t_q], vec.tensor_scalar, T.qm[:], T.qc[:], -2704.0, None, ALU.add)
+    t_pj = {0: V([t_hz], vec.quantize_mx, T.pj0[:], T.pjs0[:], T.hz[:])}
+
+    t_z3 = V([t_z1], vec.tensor_scalar, T.z3[:], T.z1[:], 3.0, None, ALU.mult)
+    t_e1, t_e3 = [], []
+    for i in range(4):
+        t_e1.append(V([t_z1], vec.quantize_mx, T.e1[:, 128 * i:128 * i + 128], T.e1s[:, 128 * i:128 * i + 128], T.z1[:, 3 - i:515 - i]))
+    for i in range(4):
+        t_e3.append(V([t_z3], vec.quantize_mx, T.e3[:, 128 * i:128 * i + 128], T.e3s[:, 128 * i:128 * i + 128], T.z3[:, 3 - i:515 - i]))
+
+    t_tr = [[] for _ in range(4 * R)]
+
+    def tr_codes(b, k, dep):
+        t_tr[4 * b + k].append(V([dep, t_rep[b]], vec.tensor_copy, w32("tr%d" % b, 128 * k, 128 * k + 128),
+                                 w32("xq", 0, 256 if b else 128).indirect(T["rep%d" % b][:, 8 * k:8 * k + 8])))
+
+    def tr_scales(b, k, dep):
+        t_tr[4 * b + k].append(A([dep, t_rep[b]], act.activation, T["trs%d" % b][:, 128 * k:128 * k + 128],
+                                 T.xqs[:, 0:256 if b else 128].indirect(T["rep%d" % b][:, 8 * k:8 * k + 8]), ACTF.Copy))
+
+    t_x0 = V([lx0], vec.quantize_mx, T.xq[:, 0:128], T.xqs[:, 0:128], T.xt[:, 0:512])
+    for k in range(4):
+        tr_codes(0, k, t_x0)
+        tr_scales(0, k, t_x0)
+    lw = dma("S", [lk], "lw", T.wt[:], T.w[:])
+    t_tab = [V([lk], vec.quantize_mx, T.win0[:, 0:256], T.wins0[:, 0:256], T.kt[:])]
+
+    cst, t_maps = {}, {}
+
+    def make_diag():
+        cst["diag"] = V([t_c16, t_q], vec.tensor_scalar, T.diag[:], T.c16[:], T.qc[:], None, ALU.is_equal)
+
+    def make_rows():
+        cst["base"] = V([cst["diag"], t_row], vec.tensor_tensor, T.base[:], T.diag[:], T.row[:, 0:320], ALU.mult)
+        t_m = V([t_iq], vec.tensor_scalar, T.mk[:], T.iq[:], T.qc[:], 2000.0, ALU.is_equal, ALU.mult)
+        t_m = V([t_m, t_qm], vec.tensor_scalar, T.mk[:, 64:260:65], T.iq[:, 64:260:65], -1.0, T.qm[:], ALU.mult, ALU.add)
+        cst["mk"] = V([t_m], vec.tensor_scalar, T.mk[:, 65:260:65], T.iq[:, 65:260:65], 0.0, -5000.0, ALU.mult, ALU.add)
+        cst["rs"] = V([t_c16], vec.tensor_scalar, T.rs[:], T.c16[:, 0:256], 0.0, None, ALU.is_gt)
+
+    def make_maps(b):
+        A([cst["diag"]], act.activation, T["mi%d" % b][:], T.diag[:], ACTF.Copy, scale=0.0)
+        A([cst["diag"]], act.activation, T["mc%d" % b][:], T.diag[:], ACTF.Copy)
+        t_maps[b] = A([cst["base"]], act.activation, T["ml%d" % b][:], T.base[:], ACTF.Copy)
+
+    def first_match(eq, rr, deps):
+        return [V(deps, vec.tensor_scalar, T[eq][:, 65 * k:65 * k + 64], T[rr][:], T[eq][:, 65 * k + 64:65 * k + 65], 1024.0,
+                  ALU.is_equal, ALU.mult) for k in range(4)]
+
+    def first_scan(eq, ds, out, deps):
+        t = V(deps + [cst["mk"]], vec.tensor_tensor_scan, T[ds][:], T.mk[:], T[eq][:], 0.0, ALU.add, ALU.max)
+        return V([t], vec.tensor_copy, T[out][:], T[ds][:, 64:260:65])
+
+    for b in range(R):
+        W, PJ, TR = ("win%d" % b, "wins%d" % b), ("pj%d" % b, "pjs%d" % b), ("tr%d" % b, "trs%d" % b)
+        wb, wa, ub, ua, jl, ll = [T["%s%d" % (n, b)] for n in ("wb", "wa", "ub", "ua", "jl", "ll")]
+        mi, mc, ml, rb = [T["%s%d" % (n, b)] for n in ("mi", "mc", "ml", "rb")]
+        dst = T.cores[rank ^ (1 << b)]
+        rid, pid, _s = topo.addr(dst)
+        mask = topo.mask(core, dst)
+        neng = len(topo.engines(core, dst))
+        E1, E3, XQ = ("e1", "e1s"), ("e3", "e3s"), ("xq", "xqs")
+
+        t_s = [mx(t_tab + t_tr[4 * b + k], T.ps[:, 512 * k:512 * k + 256], TR, 128 * k, W, 0, 256, True, True) for k in range(4)]
+        t_w = []
+        for k in range(4):
+            pm = T["pm%d" % k]
+            t = V([t_s[k], t_neg], vec.tensor_tensor_scan, pm[:], T.ps[:, 512 * k:512 * k + 256], T.neg[:], -1.0e29, ALU.max, ALU.max)
+            t_w.append(A([t], act.activation, T["sg%d" % k][:], pm[:], ACTF.Sign, bias=pm[:, 255:256], scale=-1.0,
+                         accum_out=T.eqb[:, 65 * k + 64:65 * k + 65]))
+        if b == 0:
+            t_x1 = V([lx1, t_xz], vec.quantize_mx, T.xq[:, 128:256], T.xqs[:, 128:256], T.xt[:, 512:1024])
+            make_diag()
+        if b == 1:
+            tr_codes(2, 0, t_x1)
+        for i in range(4):
+            mx([t_e1[i]] + ([t_x1, t_cm] if b else [t_x0]), T.pd[:, 512 * i:512 * i + 128], E1, 128 * i, XQ, NT * b, 128, True, False)
+        t_wb = V(t_w, vec.tensor_copy, wb[:], T.eqb[:, 64:260:65])
+
+        need("G", [t_wb])
+        g.remote_dma(wa[:], wb[:], T.sem["rl%d" % b], T.sem.loc, pid, rid, mask)
+
+        t_p = pick(PJ, 0, 64, W, 0, 256, wb[:], [t_wb, t_pj[b]])
+        t_rb = A([t_wb, t_row], act.activation, rb[:], T.row[:, 0:256].indirect(wb[:]), ACTF.Copy)
+        t_d = [mx([t_e3[i]] + t_p, T.pd[:, 512 * i:512 * i + 128], E3, 128 * i, PJ, 0, 128, False, True) for i in range(4)]
+        for i in range(4):
+            t_cs = A([t_d[i], t_hs], act.activation, T.hs[:, i:256:4], T.pd[:, 512 * i:512 * i + 64], ACTF.Copy, scale=0.25)
+        if b == 0:
+            tr_codes(1, 0, t_x1)
+            tr_codes(1, 1, t_x1)
+            t_pj[1] = V([t_hz], vec.quantize_mx, T.pj1[:], T.pjs1[:], T.hz[:])
+        else:
+            ts = first_match("eqb", "rb%d" % b, [t_rb] + t_w)
+        t_n = V([t_cs], vec.quantize_mx, T[W[0]][:, 320:448], T[W[1]][:, 320:448], T.hs[:])
+        need("G", [t_n])
+        g.remote_dma(w8(W[0], 256, 320), w8(W[0], 320, 384), T.sem["rd%d" % b], T.sem.loc, pid, rid, mask)
+        g.remote_dma(T[W[1]][:, 256:320], T[W[1]][:, 320:384], T.sem["rd%d" % b], T.sem.loc, pid, rid, mask)
+
+        if b == 0:
+            make_rows()
+            make_maps(0)
+            ts = first_match("eqb", "rb0", [t_rb] + t_w)
+        t_ub = first_scan("eqb", "dsb", ub, ts) if False else None
+        t = V(ts + [cst["mk"]], vec.tensor_tensor_scan, T.dsb[:], T.mk[:], T.eqb[:], 0.0, ALU.add, ALU.max)
+        t_ub = V([t], vec.tensor_copy, ub[:], T.dsb[:, 64:260:65])
+        t_mi = V([t_ub, t_maps[b], t_row], vec.tensor_copy, mi[:].indirect(ub[:]), T.row[:, 0:64])
+        t2 = V([t_ub], vec.tensor_scalar, T.t2[:], T.diag[:].indirect(ub[:]), 2.0, None, ALU.mult)
+        t3 = V([t_ub], vec.tensor_tensor, T.t3[:], T.diag[:].indirect(ub[:]), T.row[:, 320:384], ALU.mult)
+        t_mc = V([t2], vec.tensor_copy, mc[:].indirect(ub[:]), T.t2[:])
+        t_ml = V([t3], vec.tensor_copy, ml[:].indirect(ub[:]), T.t3[:])
+        if b + 1 < R:
+            for k in range(4):
+                tr_scales(b + 1, k, t_x1)
+            if b == 0:
+                tr_codes(1, 2, t_x1)
+            else:
+                t_pj[2] = V([t_hz], vec.quantize_mx, T.pj2[:], T.pjs2[:], T.hz[:])
+                tr_codes(2, 1, t_x1)
+                tr_codes(2, 2, t_x1)
+            make_maps(b + 1)
+        else:
+            t_wq = V([lw], vec.quantize_mx, T.wq[:], T.wqs[:], T.wt[:])
+
+        arr_l = ("rl%d" % b, neng, {})
+        t_ra = A([arr_l, t_row], act.activation, T.ra[:], T.row[:, 0:256].indirect(wa[:]), ACTF.Copy)
+        t = V([arr_l, t_mi], vec.tensor_tensor, T.g1[:], mi[:].indirect(wa[:]), T.diag[:, 0:64], ALU.mult)
+        t_wf = V([arr_l], vec.tensor_copy, T.eqa[:, 64:260:65], wa[:])
+        t = V([t, cst["rs"]], vec.tensor_tensor_scan, T.s1[:], T.rs[:, 0:64], T.g1[:], 0.0, ALU.mult, ALU.add)
+        t_jl = V([t], vec.tensor_copy, jl[:], T.s1[:, 15:64:16])
+        t_j = pick(PJ, 64, 128, W, 320, 384, jl[:], [t_jl])
+        for i in range(4):
+            mx([t_cs] + t_j, T.pd[:, 512 * i:512 * i + 128], E1, 128 * i, PJ, 0, 128, True, False)
+        arr_d = ("rd%d" % b, 2 * neng, {})
+        t_d = [mx([arr_d], T.pd[:, 512 * i:512 * i + 128], E1, 128 * i, W, 192, 128, False, True) for i in range(4)]
+        for i in range(4):
+            t_cm = A([t_d[i], t_hm], act.activation, T.hm[:, i:512:8], T.pd[:, 512 * i + 64:512 * i + 128], ACTF.Copy, scale=0.5)
+
+        ts = first_match("eqa", "ra", [t_ra, t_wf])
+        t = V(ts, vec.tensor_tensor_scan, T.dsa[:], T.mk[:], T.eqa[:], 0.0, ALU.add, ALU.max)
+        t_ua = V([t], vec.tensor_copy, ua[:], T.dsa[:, 64:260:65])
+        t = V([t_ua, t_mc], vec.tensor_tensor, T.va[:], mc[:].indirect(ua[:]), T.row[:, 256:320], ALU.mult)
+        t = V([t, t_ml], vec.tensor_copy, ml[:].indirect(ua[:]), T.va[:])
+        t = V([t], vec.tensor_tensor_scan, T.ls[:], T.rs[:], ml[:, 0:256], 0.0, ALU.mult, ALU.add)
+        t_ll = V([t], vec.tensor_copy, ll[:], T.ls[:, 15:256:16])
+        if b + 1 < R:
+            tr_codes(b + 1, 3, t_x1)
+        t_m = V([t_cm], vec.quantize_mx, T[W[0]][:, 512:640], T[W[1]][:, 512:640], T.hm[:])
+        K = ("win%d" % (b + 1), "wins%d" % (b + 1)) if b + 1 < R else ("k3", "k3s")
+        t_tab = pick(K, 0, 256, W, 0, 640, ll[:], [t_m, t_ll])
+        dma("S", [t_rb], "st", T.ch[b:b + 1, 0:NT], rb[0:1, :])
+
+    dma("S", t_tab[0:1], "st", T.oc[:], w8("k3", 0, 256))
+    for k in range(4):
+        dma("S", t_tab[1:2], "st", T.osc[4 * k:4 * k + 4, :], T.k3s[32 * k:32 * k + 4, :])
+    t_y = [mx([t_wq] + t_tab, T.ps[:, 512 * m:512 * m + 128], ("wq", "wqs"), 0, ("k3", "k3s"), 128 * m, 128, True, True) for m in range(2)]
+    t_ya = A([t_y[0]], act.activation, T.yt[:, 0:128], T.ps[:, 0:128], ACTF.Copy)
+    t_yv = V([t_y[1]], vec.tensor_copy, T.yt[:, 128:256], T.ps[:, 512:640])
+    dma("A", [t_ya, t_yv], "st", T.y[:], T.yt[:])
+    g.sync.wait_ge(T.sem.st, 16 * (R + 6))
+    g.wait_ge(T.sem.loc, 3 * R * neng)

@@ -6,26 +6,27 @@ R = 3
 NT = 64
 
 X4 = "float8_e4m3fn_x4"
-SCRATCH = {"ps": ("psum", [128, 2048], "float32"), "pd": ("psum", [128, 2048], "float32"),
+SCRATCH = {"ps": ("psum", [128, 1024], "float32"), "pd": ("psum", [128, 2048], "float32"),
            "pidx": ("sbuf", [128, 1], "int32"), "pand": ("sbuf", [128, 1], "int32")}
-for _n, _w in (("xt", 1024), ("kt", 1024), ("wt", 512), ("ones", 516), ("z1", 516), ("z3", 516), ("hs", 512), ("hm", 512),
-               ("hz", 512), ("sg0", 256), ("sg1", 256), ("sg2", 256), ("sg3", 256)):
+for _n, _w in (("xt", 1024), ("kt", 1024), ("wt", 512), ("z1", 516), ("hs", 512), ("hm", 512), ("hz", 516), ("sg0", 256), ("sg1", 256)):
     SCRATCH[_n] = ("sbuf", [128, _w], "bfloat16")
-for _n, _w in (("qc", 1), ("qm", 1), ("repi", 32), ("c16", 320), ("row", 384), ("iq", 260), ("mk", 260), ("diag", 320),
-               ("rs", 256), ("base", 320), ("neg", 256), ("pm0", 256), ("pm1", 256), ("pm2", 256), ("pm3", 256),
-               ("eqb", 260), ("eqa", 260), ("dsb", 260), ("dsa", 260), ("ra", 64), ("g1", 64), ("s1", 64), ("t2", 64),
-               ("t3", 64), ("va", 64), ("ls", 256), ("yt", 256)):
+for _n, _w in (("qc", 1), ("qm", 1), ("repi", 16), ("c16", 256), ("row", 384), ("iq", 260), ("mk", 260), ("diag", 256),
+               ("rs", 256), ("base", 256), ("neg", 256), ("pm0", 256), ("pm1", 256), ("tinb", 64), ("tina", 64),
+               ("toutb", 64), ("touta", 64), ("wrb", 64), ("wra", 64), ("nwb", 4), ("nwa", 4), ("eqb", 260), ("eqa", 260),
+               ("dsb", 260), ("dsa", 260), ("ra", 64), ("g1", 64), ("s1", 64), ("t2", 64), ("t3", 64), ("va", 64), ("mi", 320),
+               ("ls", 256), ("yt", 256), ("dk0", 256), ("dk1", 256), ("dk2", 256), ("dk3", 256),
+               ("tk0", 192), ("tk1", 192), ("tk2", 192), ("tk3", 192)):
     SCRATCH[_n] = ("sbuf", [128, _w], "float32")
-for _n, _w in (("e1", 512), ("e3", 512), ("xq", 256), ("wq", 128), ("k3", 256)):
+for _n, _w in (("e1", 512), ("xq", 256), ("wq", 128), ("k3", 256)):
     SCRATCH[_n] = ("sbuf", [128, _w], X4)
     SCRATCH[_n + "s"] = ("sbuf", [128, _w], "uint8")
 for _b in range(R):
-    for _n, _w in (("win", 640), ("pj", 128), ("tr", 512)):
+    for _n, _w in (("win", 640), ("pj", 128), ("tr", 256)):
         SCRATCH["%s%d" % (_n, _b)] = ("sbuf", [128, _w], X4)
         SCRATCH["%ss%d" % (_n, _b)] = ("sbuf", [128, _w], "uint8")
-    for _n, _w in (("rep", 32), ("wb", 4), ("wa", 4), ("ub", 4), ("ua", 4), ("jl", 4), ("ll", 16)):
+    for _n, _w in (("rep", 16), ("wb", 4), ("wa", 4), ("ub", 4), ("ua", 4), ("jl", 4), ("ll", 16)):
         SCRATCH["%s%d" % (_n, _b)] = ("sbuf", [128, _w], "uint16")
-    for _n, _w in (("mi", 320), ("mc", 320), ("ml", 320), ("rb", 64)):
+    for _n, _w in (("mc", 320), ("ml", 320), ("rb", 64), ("wcb", 2), ("wca", 2)):
         SCRATCH["%s%d" % (_n, _b)] = ("sbuf", [128, _w], "float32")
 
 SEMAPHORES = ["cv", "ca", "cp", "cg", "lx0", "lx1", "lk", "lw", "st", "loc"]
@@ -66,12 +67,15 @@ def rank_program(g, core, T, topo):
     def V(deps, fn, *args, **kw):
         return do("V", deps, fn, *args, **kw)
 
-    def A(deps, fn, *args, **kw):
-        return do("A", deps, fn, *args, **kw)
+    def A(deps, out, in_, func=ACTF.Copy, **kw):
+        return do("A", deps, act.activation, out, in_, func, **kw)
 
     def mx(deps, bank, st, a, mv, c, n, start, stop):
         return do("P", deps, ten.matmul_mx, bank, T[st[0]][:, a:a + 128], T[st[1]][:, a:a + 128],
                   T[mv[0]][:, c:c + n], T[mv[1]][:, c:c + n], start, stop)
+
+    def pd(t, a, b):
+        return T.pd[:, 512 * t + a:512 * t + b]
 
     def w8(name, a, b):
         return T[name][:, a:b].bitcast(dt.uint8)
@@ -81,186 +85,195 @@ def rank_program(g, core, T, topo):
 
     def pick(out, a, b, win, c, d, off, deps):
         tc = V(deps, vec.tensor_copy, w32(out[0], a, b), w32(win[0], c, d).indirect(off))
-        ts = A(deps, act.activation, T[out[1]][:, a:b], T[win[1]][:, c:d].indirect(off), ACTF.Copy)
+        ts = A(deps, T[out[1]][:, a:b], T[win[1]][:, c:d].indirect(off))
         return [tc, ts]
 
-    lx0 = dma("S", [], "lx0", T.xt[:, 0:512], T.x[:, 0:512])
-    lk = dma("A", [], "lk", T.kt[:], T.kb[:])
-    lx1 = dma("S", [], "lx1", T.xt[:, 512:768], T.x[:, 512:768])
+    E1, XQ = ("e1", "e1s"), ("xq", "xqs")
 
-    t_ones = V([], vec.memset, T.ones[:], 1.0)
+    lx0 = dma("S", [], "lx0", T.xt[:, 0:256], T.x[:, 0:256])
+    lk = dma("A", [], "lk", T.kt[:], T.kb[:])
+    lx1 = dma("S", [], "lx1", T.xt[:, 512:1024], T.x[:, 256:768])
+
+    t_hz = V([], vec.memset, T.hz[:], 0.0)
     t_pidx = do("G", [], g.iota, T.pidx[:], [[0, 1]], 0, 1)
-    t_repi = do("G", [], g.iota, T.repi[:], [[16, 4], [0, 8]], 0, 0, allow_small_or_imprecise_dtypes=True)
-    t_z1 = do("G", [t_ones], g.affine_select, T.z1[:], T.ones[:], [[-1, 516]], ALU.is_equal, 0.0, 3, 4)
-    t_c16 = do("G", [], g.iota, T.c16[:], [[0, 20], [1, 16]], 0, 0, allow_small_or_imprecise_dtypes=True)
+    t_repi = do("G", [], g.iota, T.repi[:], [[32, 2], [0, 4], [16, 2]], 0, 0, allow_small_or_imprecise_dtypes=True)
+    t_z1 = do("G", [t_hz], g.affine_select, T.z1[:], T.hz[:], [[-1, 516]], ALU.not_equal, 1.0, 3, 4)
+    t_c16 = do("G", [], g.iota, T.c16[:], [[0, 16], [1, 16]], 0, 0, allow_small_or_imprecise_dtypes=True)
     t_row = do("G", [], g.iota, T.row[:], [[1, 384]], 0, 0, allow_small_or_imprecise_dtypes=True)
     t_iq = do("G", [], g.iota, T.iq[:], [[-16, 4], [1, 65]], 0, 0, allow_small_or_imprecise_dtypes=True)
 
+    t_xz = A([t_hz], T.xt[:, 256:512], T.hz[:, 0:256])
+    t_hs = A([], T.hs[:], T.hz[:, 0:512])
+    t_hm = A([], T.hm[:], T.hz[:, 0:512])
     t_and = V([t_pidx], vec.tensor_scalar, T.pand[:], T.pidx[:], 15, None, ALU.bitwise_and)
-    t_hz = V([], vec.memset, T.hz[:], 0.0)
-    t_q = V([t_and], vec.tensor_copy, T.qc[:], T.pand[:])
-    t_xz = V([], vec.memset, T.xt[:, 768:1024], 0.0)
-    t_rep = [V([t_q, t_repi], vec.tensor_scalar, T["rep%d" % b][:], T.repi[:], T.qc[:], float(NT * b), ALU.add, ALU.add)
-             for b in range(R)]
-    t_hs = V([], vec.memset, T.hs[:], 0.0)
-    t_hm = V([], vec.memset, T.hm[:], 0.0)
     t_neg = V([], vec.memset, T.neg[:], -1.0e29)
-    t_qm = V([t_q], vec.tensor_scalar, T.qm[:], T.qc[:], -2704.0, None, ALU.add)
-    t_pj = {0: V([t_hz], vec.quantize_mx, T.pj0[:], T.pjs0[:], T.hz[:])}
+    t_q = V([t_and], vec.tensor_copy, T.qc[:], T.pand[:])
+    t_rep, t_pj, t_e1 = {}, {}, []
 
-    t_z3 = V([t_z1], vec.tensor_scalar, T.z3[:], T.z1[:], 3.0, None, ALU.mult)
-    t_e1, t_e3 = [], []
+    def make_rep(b):
+        t_rep[b] = V([t_q, t_repi], vec.tensor_scalar, T["rep%d" % b][:], T.repi[:], T.qc[:], float((0, 128, 192)[b]), ALU.add, ALU.add)
+
+    def make_pj(b):
+        t_pj[b] = V([t_hz], vec.quantize_mx, T["pj%d" % b][:], T["pjs%d" % b][:], T.hz[:, 0:512])
+
+    make_pj(0)
+    make_rep(0)
     for i in range(4):
         t_e1.append(V([t_z1], vec.quantize_mx, T.e1[:, 128 * i:128 * i + 128], T.e1s[:, 128 * i:128 * i + 128], T.z1[:, 3 - i:515 - i]))
-    for i in range(4):
-        t_e3.append(V([t_z3], vec.quantize_mx, T.e3[:, 128 * i:128 * i + 128], T.e3s[:, 128 * i:128 * i + 128], T.z3[:, 3 - i:515 - i]))
+    t_diag = V([t_c16, t_q], vec.tensor_scalar, T.diag[:], T.c16[:], T.qc[:], None, ALU.is_equal)
 
-    t_tr = [[] for _ in range(4 * R)]
+    t_tr = [[] for _ in range(2 * R)]
+    t_tk = {}
 
-    def tr_codes(b, k, dep):
-        t_tr[4 * b + k].append(V([dep, t_rep[b]], vec.tensor_copy, w32("tr%d" % b, 128 * k, 128 * k + 128),
-                                 w32("xq", 0, 256 if b else 128).indirect(T["rep%d" % b][:, 8 * k:8 * k + 8])))
+    def tr_codes(b, h, dep):
+        t_tr[2 * b + h].append(V([dep, t_rep[b]], vec.tensor_copy, w32("tr%d" % b, 128 * h, 128 * h + 128),
+                                 w32("xq", 0, 256 if b else 128).indirect(T["rep%d" % b][:, 8 * h:8 * h + 8])))
 
-    def tr_scales(b, k, dep):
-        t_tr[4 * b + k].append(A([dep, t_rep[b]], act.activation, T["trs%d" % b][:, 128 * k:128 * k + 128],
-                                 T.xqs[:, 0:256 if b else 128].indirect(T["rep%d" % b][:, 8 * k:8 * k + 8]), ACTF.Copy))
+    def tr_scales(b, h, dep):
+        t_tr[2 * b + h].append(A([dep, t_rep[b]], T["trs%d" % b][:, 128 * h:128 * h + 128],
+                                 T.xqs[:, 0:256 if b else 128].indirect(T["rep%d" % b][:, 8 * h:8 * h + 8])))
 
-    t_x0 = V([lx0], vec.quantize_mx, T.xq[:, 0:128], T.xqs[:, 0:128], T.xt[:, 0:512])
-    for k in range(4):
-        tr_codes(0, k, t_x0)
-        tr_scales(0, k, t_x0)
+    def unpack_tokens(c, o, n, deps):
+        ts = [mx(deps + [t_e1[t]], pd(t, 0, 128), E1, 128 * t, XQ, c, 128, True, True) for t in range(4)]
+        return [A([ts[t]], T["tk%d" % t][:, o:o + n], pd(t, 0, n), scale=0.25) for t in range(4)]
+
+    t_x0 = V([lx0, t_xz], vec.quantize_mx, T.xq[:, 0:128], T.xqs[:, 0:128], T.xt[:, 0:512])
+    for h in range(2):
+        tr_codes(0, h, t_x0)
+        tr_scales(0, h, t_x0)
+    t_tk[0] = unpack_tokens(0, 0, 64, [t_x0])
+    t_rs = V([t_c16], vec.tensor_scalar, T.rs[:], T.c16[:], 0.0, None, ALU.is_gt)
     lw = dma("S", [lk], "lw", T.wt[:], T.w[:])
     t_tab = [V([lk], vec.quantize_mx, T.win0[:, 0:256], T.wins0[:, 0:256], T.kt[:])]
 
     cst, t_maps = {}, {}
 
-    def make_diag():
-        cst["diag"] = V([t_c16, t_q], vec.tensor_scalar, T.diag[:], T.c16[:], T.qc[:], None, ALU.is_equal)
-
     def make_rows():
-        cst["base"] = V([cst["diag"], t_row], vec.tensor_tensor, T.base[:], T.diag[:], T.row[:, 0:320], ALU.mult)
-        t_m = V([t_iq], vec.tensor_scalar, T.mk[:], T.iq[:], T.qc[:], 2000.0, ALU.is_equal, ALU.mult)
+        t_m = V([t_iq], vec.tensor_scalar, T.mk[:], T.iq[:], T.qc[:], -2000.0, ALU.is_equal, ALU.mult)
+        t_qm = V([t_q], vec.tensor_scalar, T.qm[:], T.qc[:], 2000.0, None, ALU.add)
+        cst["base"] = V([t_diag, t_row], vec.tensor_tensor, T.base[:], T.diag[:], T.row[:, 0:256], ALU.mult)
         t_m = V([t_m, t_qm], vec.tensor_scalar, T.mk[:, 64:260:65], T.iq[:, 64:260:65], -1.0, T.qm[:], ALU.mult, ALU.add)
-        cst["mk"] = V([t_m], vec.tensor_scalar, T.mk[:, 65:260:65], T.iq[:, 65:260:65], 0.0, -5000.0, ALU.mult, ALU.add)
-        cst["rs"] = V([t_c16], vec.tensor_scalar, T.rs[:], T.c16[:, 0:256], 0.0, None, ALU.is_gt)
+        cst["mk"] = V([t_m], vec.tensor_scalar, T.mk[:, 65:260:65], T.iq[:, 65:260:65], 0.0, 100000.0, ALU.mult, ALU.add)
 
     def make_maps(b):
-        A([cst["diag"]], act.activation, T["mi%d" % b][:], T.diag[:], ACTF.Copy, scale=0.0)
-        A([cst["diag"]], act.activation, T["mc%d" % b][:], T.diag[:], ACTF.Copy)
-        t_maps[b] = A([cst["base"]], act.activation, T["ml%d" % b][:], T.base[:], ACTF.Copy)
+        if b == 0:
+            A([t_diag], T.mi[:, 64:320], T.diag[:], scale=0.0)
+        A([t_diag], T["mc%d" % b][:, 64:320], T.diag[:])
+        t_maps[b] = A([cst["base"]], T["ml%d" % b][:, 64:320], T.base[:])
 
-    def first_match(eq, rr, deps):
-        return [V(deps, vec.tensor_scalar, T[eq][:, 65 * k:65 * k + 64], T[rr][:], T[eq][:, 65 * k + 64:65 * k + 65], 1024.0,
-                  ALU.is_equal, ALU.mult) for k in range(4)]
+    def squares(eq, wr, nw, rr, t_wr, t_w):
+        t_c = A([t_wr], T[eq][:, 64:260:65], T[wr][:, 15:64:16])
+        t_n = A([t_wr], T[nw][:], T[wr][:, 15:64:16], scale=-64.0)
+        t_r = A([t_w, t_row], T[rr][:], T.row[:, 0:256].indirect(t_list[eq]))
+        return t_r, [t_c] + [A([t_n, t_r], T[eq][:, 65 * k:65 * k + 64], T[rr][:], ACTF.Square, bias=T[nw][:, k:k + 1], scale=64.0)
+                             for k in range(4)]
 
-    def first_scan(eq, ds, out, deps):
-        t = V(deps + [cst["mk"]], vec.tensor_tensor_scan, T[ds][:], T.mk[:], T[eq][:], 0.0, ALU.add, ALU.max)
-        return V([t], vec.tensor_copy, T[out][:], T[ds][:, 64:260:65])
-
+    t_list = {}
     for b in range(R):
         W, PJ, TR = ("win%d" % b, "wins%d" % b), ("pj%d" % b, "pjs%d" % b), ("tr%d" % b, "trs%d" % b)
         wb, wa, ub, ua, jl, ll = [T["%s%d" % (n, b)] for n in ("wb", "wa", "ub", "ua", "jl", "ll")]
-        mi, mc, ml, rb = [T["%s%d" % (n, b)] for n in ("mi", "mc", "ml", "rb")]
+        mc, ml, rb, wcb, wca = [T["%s%d" % (n, b)] for n in ("mc", "ml", "rb", "wcb", "wca")]
+        t_list["eqb"], t_list["eqa"] = wb[:], wa[:]
         dst = T.cores[rank ^ (1 << b)]
         rid, pid, _s = topo.addr(dst)
         mask = topo.mask(core, dst)
         neng = len(topo.engines(core, dst))
-        E1, E3, XQ = ("e1", "e1s"), ("e3", "e3s"), ("xq", "xqs")
 
-        t_s = [mx(t_tab + t_tr[4 * b + k], T.ps[:, 512 * k:512 * k + 256], TR, 128 * k, W, 0, 256, True, True) for k in range(4)]
-        t_w = []
-        for k in range(4):
-            pm = T["pm%d" % k]
-            t = V([t_s[k], t_neg], vec.tensor_tensor_scan, pm[:], T.ps[:, 512 * k:512 * k + 256], T.neg[:], -1.0e29, ALU.max, ALU.max)
-            t_w.append(A([t], act.activation, T["sg%d" % k][:], pm[:], ACTF.Sign, bias=pm[:, 255:256], scale=-1.0,
-                         accum_out=T.eqb[:, 65 * k + 64:65 * k + 65]))
+        t_s = [mx(t_tab + t_tr[2 * b + h], T.ps[:, 512 * h:512 * h + 256], TR, 128 * h, W, 0, 256, True, True) for h in range(2)]
+        t_u = [mx([t_e1[t]] + ([t_cm] if b else t_tk[0]), pd(t, 0, 256), E1, 128 * t, W, 0, 256, True, True) for t in range(4)]
         if b == 0:
-            t_x1 = V([lx1, t_xz], vec.quantize_mx, T.xq[:, 128:256], T.xqs[:, 128:256], T.xt[:, 512:1024])
-            make_diag()
-        if b == 1:
+            make_pj(1)
+            make_pj(2)
+        elif b == 1:
             tr_codes(2, 0, t_x1)
-        for i in range(4):
-            mx([t_e1[i]] + ([t_x1, t_cm] if b else [t_x0]), T.pd[:, 512 * i:512 * i + 128], E1, 128 * i, XQ, NT * b, 128, True, False)
-        t_wb = V(t_w, vec.tensor_copy, wb[:], T.eqb[:, 64:260:65])
-
-        need("G", [t_wb])
-        g.remote_dma(wa[:], wb[:], T.sem["rl%d" % b], T.sem.loc, pid, rid, mask)
-
-        t_p = pick(PJ, 0, 64, W, 0, 256, wb[:], [t_wb, t_pj[b]])
-        t_rb = A([t_wb, t_row], act.activation, rb[:], T.row[:, 0:256].indirect(wb[:]), ACTF.Copy)
-        t_d = [mx([t_e3[i]] + t_p, T.pd[:, 512 * i:512 * i + 128], E3, 128 * i, PJ, 0, 128, False, True) for i in range(4)]
-        for i in range(4):
-            t_cs = A([t_d[i], t_hs], act.activation, T.hs[:, i:256:4], T.pd[:, 512 * i:512 * i + 64], ACTF.Copy, scale=0.25)
-        if b == 0:
-            tr_codes(1, 0, t_x1)
-            tr_codes(1, 1, t_x1)
-            t_pj[1] = V([t_hz], vec.quantize_mx, T.pj1[:], T.pjs1[:], T.hz[:])
+            tr_codes(2, 1, t_x1)
         else:
-            ts = first_match("eqb", "rb%d" % b, [t_rb] + t_w)
-        t_n = V([t_cs], vec.quantize_mx, T[W[0]][:, 320:448], T[W[1]][:, 320:448], T.hs[:])
+            t_wq = V([lw], vec.quantize_mx, T.wq[:], T.wqs[:], T.wt[:])
+        t_w = []
+        for h in range(2):
+            pm = T["pm%d" % h]
+            t = V([t_s[h], t_neg], vec.tensor_tensor_scan, pm[:], T.ps[:, 512 * h:512 * h + 256], T.neg[:], -1.0e29, ALU.max, ALU.max)
+            t_w.append(A([t], T["sg%d" % h][:], pm[:], ACTF.Sign, bias=pm[:, 255:256], scale=-1.0, accum_out=wcb[:, h:h + 1]))
+        need("G", t_w)
+        g.remote_dma(wca[:], wcb[:], T.sem["rl%d" % b], T.sem.loc, pid, rid, mask)
+
+        t = V([t_w[0], t_diag], vec.tensor_scalar, T.tinb[:, 0:32], T.diag[:, 0:32], wcb[:, 0:1], None, ALU.mult)
+        t_dk = [V([t_u[0]], vec.tensor_scalar, T.dk0[:], pd(0, 0, 256), 0.75, None, ALU.mult)]
+        for i in (1, 2, 3):
+            t_dk.append(A([t_u[i]], T["dk%d" % i][:], pd(i, 0, 256), scale=0.75))
+        t1 = V([t_w[1]], vec.tensor_scalar, T.tinb[:, 32:64], T.diag[:, 0:32], wcb[:, 1:2], None, ALU.mult)
+        t = V([t, t1], vec.transpose, T.toutb[:], T.tinb[:])
+        t_wr = V([t, t_rs], vec.tensor_tensor_scan, T.wrb[:], T.rs[:, 0:64], T.toutb[:], 0.0, ALU.mult, ALU.add)
+        t_wb = V([t_wr], vec.tensor_copy, wb[:], T.wrb[:, 15:64:16])
+
+        t_cs = [V([t_wb, t_dk[t], t_hs] + t_tk[b], vec.tensor_tensor, T.hs[:, t:256:4], T["dk%d" % t][:].indirect(wb[:]),
+                  T["tk%d" % t][:, NT * b:NT * b + NT], ALU.add) for t in range(4)]
+        t_n = V(t_cs, vec.quantize_mx, T[W[0]][:, 320:448], T[W[1]][:, 320:448], T.hs[:])
         need("G", [t_n])
         g.remote_dma(w8(W[0], 256, 320), w8(W[0], 320, 384), T.sem["rd%d" % b], T.sem.loc, pid, rid, mask)
         g.remote_dma(T[W[1]][:, 256:320], T[W[1]][:, 320:384], T.sem["rd%d" % b], T.sem.loc, pid, rid, mask)
 
+        t_rb, ts = squares("eqb", "wrb", "nwb", "rb%d" % b, t_wr, t_wb)
+        t2 = A([t_diag], T.t2[:], T.diag[:].indirect(wb[:]), scale=2.0)
         if b == 0:
             make_rows()
             make_maps(0)
-            ts = first_match("eqb", "rb0", [t_rb] + t_w)
-        t_ub = first_scan("eqb", "dsb", ub, ts) if False else None
-        t = V(ts + [cst["mk"]], vec.tensor_tensor_scan, T.dsb[:], T.mk[:], T.eqb[:], 0.0, ALU.add, ALU.max)
-        t_ub = V([t], vec.tensor_copy, ub[:], T.dsb[:, 64:260:65])
-        t_mi = V([t_ub, t_maps[b], t_row], vec.tensor_copy, mi[:].indirect(ub[:]), T.row[:, 0:64])
-        t2 = V([t_ub], vec.tensor_scalar, T.t2[:], T.diag[:].indirect(ub[:]), 2.0, None, ALU.mult)
-        t3 = V([t_ub], vec.tensor_tensor, T.t3[:], T.diag[:].indirect(ub[:]), T.row[:, 320:384], ALU.mult)
-        t_mc = V([t2], vec.tensor_copy, mc[:].indirect(ub[:]), T.t2[:])
+        t3 = V([t_row], vec.tensor_tensor, T.t3[:], T.diag[:].indirect(wb[:]), T.row[:, 320:384], ALU.mult)
+        t = V(ts + [cst["mk"]], vec.tensor_tensor_scan, T.dsb[:], T.mk[:], T.eqb[:], 100000.0, ALU.add, ALU.min)
+        t_ub = V([t], vec.tensor_scalar, ub[:], T.dsb[:, 64:260:65], 64.0, None, ALU.add)
+        if b == 0:
+            t_x1 = V([lx1], vec.quantize_mx, T.xq[:, 128:256], T.xqs[:, 128:256], T.xt[:, 512:1024])
+            make_rep(1)
+            make_rep(2)
+            t_tk[1] = t_tk[2] = unpack_tokens(128, 64, 128, [t_x1] + t_dk)
+        t_mi = V([t_ub, t_maps[b], t_row], vec.tensor_copy, T.mi[:].indirect(ub[:]), T.row[:, 0:64])
         t_ml = V([t3], vec.tensor_copy, ml[:].indirect(ub[:]), T.t3[:])
+        t_mc = V([t2], vec.tensor_copy, mc[:].indirect(ub[:]), T.t2[:])
         if b + 1 < R:
-            for k in range(4):
-                tr_scales(b + 1, k, t_x1)
-            if b == 0:
-                tr_codes(1, 2, t_x1)
-            else:
-                t_pj[2] = V([t_hz], vec.quantize_mx, T.pj2[:], T.pjs2[:], T.hz[:])
-                tr_codes(2, 1, t_x1)
-                tr_codes(2, 2, t_x1)
+            for h in range(2):
+                if b == 0:
+                    tr_codes(1, h, t_x1)
+                tr_scales(b + 1, h, t_x1)
             make_maps(b + 1)
-        else:
-            t_wq = V([lw], vec.quantize_mx, T.wq[:], T.wqs[:], T.wt[:])
 
         arr_l = ("rl%d" % b, neng, {})
-        t_ra = A([arr_l, t_row], act.activation, T.ra[:], T.row[:, 0:256].indirect(wa[:]), ACTF.Copy)
-        t = V([arr_l, t_mi], vec.tensor_tensor, T.g1[:], mi[:].indirect(wa[:]), T.diag[:, 0:64], ALU.mult)
-        t_wf = V([arr_l], vec.tensor_copy, T.eqa[:, 64:260:65], wa[:])
-        t = V([t, cst["rs"]], vec.tensor_tensor_scan, T.s1[:], T.rs[:, 0:64], T.g1[:], 0.0, ALU.mult, ALU.add)
+        ta = [A([arr_l, t_diag], T.tina[:, 32 * h:32 * h + 32], T.diag[:, 0:32], scale=wca[:, h:h + 1]) for h in range(2)]
+        t = V(ta, vec.transpose, T.touta[:], T.tina[:])
+        t_wr = V([t], vec.tensor_tensor_scan, T.wra[:], T.rs[:, 0:64], T.touta[:], 0.0, ALU.mult, ALU.add)
+        t_wa = V([t_wr], vec.tensor_copy, wa[:], T.wra[:, 15:64:16])
+        t_ra, ts = squares("eqa", "wra", "nwa", "ra", t_wr, t_wa)
+        t = V([t_wa, t_mi], vec.tensor_tensor, T.g1[:], T.mi[:, 64:320].indirect(wa[:]), T.diag[:, 0:64], ALU.mult)
+        t_va = V([t_mc], vec.tensor_tensor, T.va[:], mc[:, 64:320].indirect(wa[:]), T.row[:, 256:320], ALU.mult)
+        t = V([t], vec.tensor_tensor_scan, T.s1[:], T.rs[:, 0:64], T.g1[:], 0.0, ALU.mult, ALU.add)
         t_jl = V([t], vec.tensor_copy, jl[:], T.s1[:, 15:64:16])
-        t_j = pick(PJ, 64, 128, W, 320, 384, jl[:], [t_jl])
+        t_j = pick(PJ, 64, 128, W, 320, 384, jl[:], [t_jl, t_pj[b]])
         for i in range(4):
-            mx([t_cs] + t_j, T.pd[:, 512 * i:512 * i + 128], E1, 128 * i, PJ, 0, 128, True, False)
+            mx(t_dk + t_j + t_tk[1], pd(i, 0, 128), E1, 128 * i, PJ, 0, 128, True, False)
         arr_d = ("rd%d" % b, 2 * neng, {})
-        t_d = [mx([arr_d], T.pd[:, 512 * i:512 * i + 128], E1, 128 * i, W, 192, 128, False, True) for i in range(4)]
+        t_d = [mx([arr_d], pd(i, 0, 128), E1, 128 * i, W, 192, 128, False, True) for i in range(4)]
         for i in range(4):
-            t_cm = A([t_d[i], t_hm], act.activation, T.hm[:, i:512:8], T.pd[:, 512 * i + 64:512 * i + 128], ACTF.Copy, scale=0.5)
+            t_cm = A([t_d[i], t_hm], T.hm[:, i:512:8], pd(i, 64, 128), scale=0.5)
 
-        ts = first_match("eqa", "ra", [t_ra, t_wf])
-        t = V(ts, vec.tensor_tensor_scan, T.dsa[:], T.mk[:], T.eqa[:], 0.0, ALU.add, ALU.max)
-        t_ua = V([t], vec.tensor_copy, ua[:], T.dsa[:, 64:260:65])
-        t = V([t_ua, t_mc], vec.tensor_tensor, T.va[:], mc[:].indirect(ua[:]), T.row[:, 256:320], ALU.mult)
-        t = V([t, t_ml], vec.tensor_copy, ml[:].indirect(ua[:]), T.va[:])
-        t = V([t], vec.tensor_tensor_scan, T.ls[:], T.rs[:], ml[:, 0:256], 0.0, ALU.mult, ALU.add)
+        t = V(ts, vec.tensor_tensor_scan, T.dsa[:], T.mk[:], T.eqa[:], 100000.0, ALU.add, ALU.min)
+        t_ua = V([t], vec.tensor_scalar, ua[:], T.dsa[:, 64:260:65], 64.0, None, ALU.add)
+        t = V([t_ua, t_va, t_ml], vec.tensor_copy, ml[:].indirect(ua[:]), T.va[:])
+        t = V([t], vec.tensor_tensor_scan, T.ls[:], T.rs[:], ml[:, 64:320], 0.0, ALU.mult, ALU.add)
         t_ll = V([t], vec.tensor_copy, ll[:], T.ls[:, 15:256:16])
-        if b + 1 < R:
-            tr_codes(b + 1, 3, t_x1)
         t_m = V([t_cm], vec.quantize_mx, T[W[0]][:, 512:640], T[W[1]][:, 512:640], T.hm[:])
-        K = ("win%d" % (b + 1), "wins%d" % (b + 1)) if b + 1 < R else ("k3", "k3s")
-        t_tab = pick(K, 0, 256, W, 0, 640, ll[:], [t_m, t_ll])
         dma("S", [t_rb], "st", T.ch[b:b + 1, 0:NT], rb[0:1, :])
+        if b + 1 < R:
+            t_tab = pick(("win%d" % (b + 1), "wins%d" % (b + 1)), 0, 256, W, 0, 640, ll[:], [t_m, t_ll])
 
-    dma("S", t_tab[0:1], "st", T.oc[:], w8("k3", 0, 256))
-    for k in range(4):
-        dma("S", t_tab[1:2], "st", T.osc[4 * k:4 * k + 4, :], T.k3s[32 * k:32 * k + 4, :])
-    t_y = [mx([t_wq] + t_tab, T.ps[:, 512 * m:512 * m + 128], ("wq", "wqs"), 0, ("k3", "k3s"), 128 * m, 128, True, True) for m in range(2)]
-    t_ya = A([t_y[0]], act.activation, T.yt[:, 0:128], T.ps[:, 0:128], ACTF.Copy)
+    K = ("k3", "k3s")
+    t_h = [pick(K, 128 * m, 128 * m + 128, W, 0, 640, ll[:, 8 * m:8 * m + 8], [t_m, t_ll]) for m in range(2)]
+    t_y = [mx([t_wq] + t_h[m], T.ps[:, 512 * m:512 * m + 128], ("wq", "wqs"), 0, K, 128 * m, 128, True, True) for m in range(2)]
+    t_ya = A([t_y[0]], T.yt[:, 0:128], T.ps[:, 0:128])
+    dma("A", [t_ya], "st", T.y[:, 0:128], T.yt[:, 0:128])
     t_yv = V([t_y[1]], vec.tensor_copy, T.yt[:, 128:256], T.ps[:, 512:640])
-    dma("A", [t_ya, t_yv], "st", T.y[:], T.yt[:])
-    g.sync.wait_ge(T.sem.st, 16 * (R + 6))
+    for m in range(2):
+        dma("S", t_h[m][0:1], "st", T.oc[:, 512 * m:512 * m + 512], w8("k3", 128 * m, 128 * m + 128))
+    for k in range(4):
+        dma("AASS"[k], t_h[1][1:2], "st", T.osc[4 * k:4 * k + 4, :], T.k3s[32 * k:32 * k + 4, :])
+    dma("S", [t_yv], "st", T.y[:, 128:256], T.yt[:, 128:256])
+    g.sync.wait_ge(T.sem.st, 16 * (R + 8))
     g.wait_ge(T.sem.loc, 3 * R * neng)

@@ -6,14 +6,14 @@ R = 3
 NT = 64
 
 X4 = "float8_e4m3fn_x4"
-SCRATCH = {"ps": ("psum", [128, 1024], "float32"), "pd": ("psum", [128, 2048], "float32"),
+SCRATCH = {"ps": ("psum", [128, 1024], "float32"), "pd": ("psum", [128, 2048], "float32"), "pe": ("psum", [128, 1024], "float32"),
            "pidx": ("sbuf", [128, 1], "int32"), "pand": ("sbuf", [128, 1], "int32")}
 for _n, _w in (("xt", 1024), ("kt", 1024), ("wt", 512), ("z1", 516), ("hs", 512), ("hm", 512), ("hz", 516), ("sg0", 256), ("sg1", 256)):
     SCRATCH[_n] = ("sbuf", [128, _w], "bfloat16")
 for _n, _w in (("qc", 1), ("qm", 1), ("repi", 16), ("c16", 256), ("row", 384), ("iq", 260), ("mk", 260), ("diag", 256),
-               ("rs", 256), ("base", 256), ("neg", 256), ("pm0", 256), ("pm1", 256), ("tinb", 64), ("tina", 64),
-               ("toutb", 64), ("touta", 64), ("wrb", 64), ("wra", 64), ("nwb", 4), ("nwa", 4), ("eqb", 260), ("eqa", 260),
-               ("dsb", 260), ("dsa", 260), ("ra", 64), ("g1", 64), ("s1", 64), ("t2", 64), ("t3", 64), ("va", 64), ("mi", 320),
+               ("diagn", 32), ("rs", 256), ("base", 256), ("neg", 256), ("jmk", 256), ("step", 80), ("pm0", 256), ("pm1", 256),
+               ("tinb", 64), ("tina", 64), ("toutb", 64), ("touta", 64), ("wrb", 64), ("wra", 64), ("eqb", 260), ("eqa", 260),
+               ("eqj", 256), ("dsb", 260), ("dsa", 260), ("dsj", 256), ("ra", 64), ("t3", 64), ("va", 64), ("vd", 64),
                ("ls", 256), ("yt", 256), ("dk0", 256), ("dk1", 256), ("dk2", 256), ("dk3", 256),
                ("tk0", 192), ("tk1", 192), ("tk2", 192), ("tk3", 192)):
     SCRATCH[_n] = ("sbuf", [128, _w], "float32")
@@ -26,7 +26,7 @@ for _b in range(R):
         SCRATCH["%ss%d" % (_n, _b)] = ("sbuf", [128, _w], "uint8")
     for _n, _w in (("rep", 16), ("wb", 4), ("wa", 4), ("ub", 4), ("ua", 4), ("jl", 4), ("ll", 16)):
         SCRATCH["%s%d" % (_n, _b)] = ("sbuf", [128, _w], "uint16")
-    for _n, _w in (("mc", 320), ("ml", 320), ("rb", 64), ("wcb", 2), ("wca", 2)):
+    for _n, _w in (("ml", 320), ("rb", 64), ("wcb", 2), ("wca", 2)):
         SCRATCH["%s%d" % (_n, _b)] = ("sbuf", [128, _w], "float32")
 
 SEMAPHORES = ["cv", "ca", "cp", "cg", "lx0", "lx1", "lk", "lw", "st", "loc"]
@@ -70,12 +70,15 @@ def rank_program(g, core, T, topo):
     def A(deps, out, in_, func=ACTF.Copy, **kw):
         return do("A", deps, act.activation, out, in_, func, **kw)
 
-    def mx(deps, bank, st, a, mv, c, n, start, stop):
+    def mx(deps, bank, st, a, mv, c, n, start=True, stop=True):
         return do("P", deps, ten.matmul_mx, bank, T[st[0]][:, a:a + 128], T[st[1]][:, a:a + 128],
                   T[mv[0]][:, c:c + n], T[mv[1]][:, c:c + n], start, stop)
 
     def pd(t, a, b):
         return T.pd[:, 512 * t + a:512 * t + b]
+
+    def px(t, a, b):
+        return (T.ps, T.pe)[t // 2][:, 512 * (t % 2) + a:512 * (t % 2) + b]
 
     def w8(name, a, b):
         return T[name][:, a:b].bitcast(dt.uint8)
@@ -93,21 +96,23 @@ def rank_program(g, core, T, topo):
     lx0 = dma("S", [], "lx0", T.xt[:, 0:256], T.x[:, 0:256])
     lk = dma("A", [], "lk", T.kt[:], T.kb[:])
     lx1 = dma("S", [], "lx1", T.xt[:, 512:1024], T.x[:, 256:768])
+    lw = dma("S", [], "lw", T.wt[:], T.w[:])
 
-    t_hz = V([], vec.memset, T.hz[:], 0.0)
+    t_z0 = V([], vec.memset, T.z1[:], 0.0)
     t_pidx = do("G", [], g.iota, T.pidx[:], [[0, 1]], 0, 1)
     t_repi = do("G", [], g.iota, T.repi[:], [[32, 2], [0, 4], [16, 2]], 0, 0, allow_small_or_imprecise_dtypes=True)
-    t_z1 = do("G", [t_hz], g.affine_select, T.z1[:], T.hz[:], [[-1, 516]], ALU.not_equal, 1.0, 3, 4)
+    t_z1 = do("G", [t_z0], g.affine_select, T.z1[:, 3:515:4], T.z1[:, 3:515:4], [[-1, 128]], ALU.not_equal, 1.0, 0, 1)
     t_c16 = do("G", [], g.iota, T.c16[:], [[0, 16], [1, 16]], 0, 0, allow_small_or_imprecise_dtypes=True)
     t_row = do("G", [], g.iota, T.row[:], [[1, 384]], 0, 0, allow_small_or_imprecise_dtypes=True)
     t_iq = do("G", [], g.iota, T.iq[:], [[-16, 4], [1, 65]], 0, 0, allow_small_or_imprecise_dtypes=True)
 
+    t_hz = V([], vec.memset, T.hz[:], 0.0)
     t_xz = A([t_hz], T.xt[:, 256:512], T.hz[:, 0:256])
-    t_hs = A([], T.hs[:], T.hz[:, 0:512])
-    t_hm = A([], T.hm[:], T.hz[:, 0:512])
     t_and = V([t_pidx], vec.tensor_scalar, T.pand[:], T.pidx[:], 15, None, ALU.bitwise_and)
-    t_neg = V([], vec.memset, T.neg[:], -1.0e29)
     t_q = V([t_and], vec.tensor_copy, T.qc[:], T.pand[:])
+    t_neg = A([t_hz], T.neg[:], T.hz[:, 0:256], ACTF.Copy, bias=-1.0e29)
+    t_jm = [A([t_hz], T.jmk[:], T.hz[:, 0:256], ACTF.Copy, bias=-1.0)]
+    t_jm.append(A(t_jm, T.jmk[:, 0:256:64], T.hz[:, 0:4], ACTF.Copy, bias=100000.0))
     t_rep, t_pj, t_e1 = {}, {}, []
 
     def make_rep(b):
@@ -115,12 +120,6 @@ def rank_program(g, core, T, topo):
 
     def make_pj(b):
         t_pj[b] = V([t_hz], vec.quantize_mx, T["pj%d" % b][:], T["pjs%d" % b][:], T.hz[:, 0:512])
-
-    make_pj(0)
-    make_rep(0)
-    for i in range(4):
-        t_e1.append(V([t_z1], vec.quantize_mx, T.e1[:, 128 * i:128 * i + 128], T.e1s[:, 128 * i:128 * i + 128], T.z1[:, 3 - i:515 - i]))
-    t_diag = V([t_c16, t_q], vec.tensor_scalar, T.diag[:], T.c16[:], T.qc[:], None, ALU.is_equal)
 
     t_tr = [[] for _ in range(2 * R)]
     t_tk = {}
@@ -133,78 +132,74 @@ def rank_program(g, core, T, topo):
         t_tr[2 * b + h].append(A([dep, t_rep[b]], T["trs%d" % b][:, 128 * h:128 * h + 128],
                                  T.xqs[:, 0:256 if b else 128].indirect(T["rep%d" % b][:, 8 * h:8 * h + 8])))
 
-    def unpack_tokens(c, o, n, deps):
-        ts = [mx(deps + [t_e1[t]], pd(t, 0, 128), E1, 128 * t, XQ, c, 128, True, True) for t in range(4)]
-        return [A([ts[t]], T["tk%d" % t][:, o:o + n], pd(t, 0, n), scale=0.25) for t in range(4)]
-
+    make_rep(0)
     t_x0 = V([lx0, t_xz], vec.quantize_mx, T.xq[:, 0:128], T.xqs[:, 0:128], T.xt[:, 0:512])
+    for i in range(4):
+        t_e1.append(V([t_z1], vec.quantize_mx, T.e1[:, 128 * i:128 * i + 128], T.e1s[:, 128 * i:128 * i + 128], T.z1[:, 3 - i:515 - i]))
+    tr_codes(0, 0, t_x0)
     for h in range(2):
-        tr_codes(0, h, t_x0)
         tr_scales(0, h, t_x0)
-    t_tk[0] = unpack_tokens(0, 0, 64, [t_x0])
-    t_rs = V([t_c16], vec.tensor_scalar, T.rs[:], T.c16[:], 0.0, None, ALU.is_gt)
-    lw = dma("S", [lk], "lw", T.wt[:], T.w[:])
     t_tab = [V([lk], vec.quantize_mx, T.win0[:, 0:256], T.wins0[:, 0:256], T.kt[:])]
-
+    tr_codes(0, 1, t_x0)
+    t_tkm = [mx([t_x0, t_e1[t]], pd(t, 0, 128), E1, 128 * t, XQ, 0, 128) for t in range(4)]
+    t_tk[0] = [A([t_tkm[t]], T["tk%d" % t][:, 0:64], pd(t, 0, 64), scale=0.25) for t in range(4)]
+    t_hs = A([], T.hs[:], T.hz[:, 0:512])
+    t_diag = V([t_c16, t_q], vec.tensor_scalar, T.diag[:], T.c16[:], T.qc[:], None, ALU.is_equal)
+    t_x1 = V([lx1], vec.quantize_mx, T.xq[:, 128:256], T.xqs[:, 128:256], T.xt[:, 512:1024])
     cst, t_maps = {}, {}
 
-    def make_rows():
+    def make_mk():
         t_m = V([t_iq], vec.tensor_scalar, T.mk[:], T.iq[:], T.qc[:], -2000.0, ALU.is_equal, ALU.mult)
         t_qm = V([t_q], vec.tensor_scalar, T.qm[:], T.qc[:], 2000.0, None, ALU.add)
-        cst["base"] = V([t_diag, t_row], vec.tensor_tensor, T.base[:], T.diag[:], T.row[:, 0:256], ALU.mult)
+        t_m1 = V([t_m], vec.tensor_scalar, T.mk[:, 65:260:65], T.iq[:, 65:260:65], 0.0, 100000.0, ALU.mult, ALU.add)
         t_m = V([t_m, t_qm], vec.tensor_scalar, T.mk[:, 64:260:65], T.iq[:, 64:260:65], -1.0, T.qm[:], ALU.mult, ALU.add)
-        cst["mk"] = V([t_m], vec.tensor_scalar, T.mk[:, 65:260:65], T.iq[:, 65:260:65], 0.0, 100000.0, ALU.mult, ALU.add)
+        cst["mk"] = [t_m1, t_m]
 
-    def make_maps(b):
-        if b == 0:
-            A([t_diag], T.mi[:, 64:320], T.diag[:], scale=0.0)
-        A([t_diag], T["mc%d" % b][:, 64:320], T.diag[:])
+    def make_ml(b):
         t_maps[b] = A([cst["base"]], T["ml%d" % b][:, 64:320], T.base[:])
 
-    def squares(eq, wr, nw, rr, t_wr, t_w):
-        t_c = A([t_wr], T[eq][:, 64:260:65], T[wr][:, 15:64:16])
-        t_n = A([t_wr], T[nw][:], T[wr][:, 15:64:16], scale=-64.0)
-        t_r = A([t_w, t_row], T[rr][:], T.row[:, 0:256].indirect(t_list[eq]))
-        return t_r, [t_c] + [A([t_n, t_r], T[eq][:, 65 * k:65 * k + 64], T[rr][:], ACTF.Square, bias=T[nw][:, k:k + 1], scale=64.0)
-                             for k in range(4)]
+    def squares(eq, n, row, wr, deps):
+        return [A(deps, T[eq][:, n * k:n * k + 64], row, ACTF.Square, bias=T[wr][:, 16 * k + 15:16 * k + 16], scale=64.0)
+                for k in range(4)]
 
-    t_list = {}
     for b in range(R):
         W, PJ, TR = ("win%d" % b, "wins%d" % b), ("pj%d" % b, "pjs%d" % b), ("tr%d" % b, "trs%d" % b)
         wb, wa, ub, ua, jl, ll = [T["%s%d" % (n, b)] for n in ("wb", "wa", "ub", "ua", "jl", "ll")]
-        mc, ml, rb, wcb, wca = [T["%s%d" % (n, b)] for n in ("mc", "ml", "rb", "wcb", "wca")]
-        t_list["eqb"], t_list["eqa"] = wb[:], wa[:]
+        ml, rb, wcb, wca = [T["%s%d" % (n, b)] for n in ("ml", "rb", "wcb", "wca")]
         dst = T.cores[rank ^ (1 << b)]
         rid, pid, _s = topo.addr(dst)
         mask = topo.mask(core, dst)
         neng = len(topo.engines(core, dst))
 
-        t_s = [mx(t_tab + t_tr[2 * b + h], T.ps[:, 512 * h:512 * h + 256], TR, 128 * h, W, 0, 256, True, True) for h in range(2)]
-        t_u = [mx([t_e1[t]] + ([t_cm] if b else t_tk[0]), pd(t, 0, 256), E1, 128 * t, W, 0, 256, True, True) for t in range(4)]
+        t_s = [mx(t_tab + t_tr[2 * b + h], T.ps[:, 512 * h:512 * h + 256], TR, 128 * h, W, 0, 256) for h in range(2)]
+        t_u = [mx([t_e1[t]] + (t_cm if b else t_tk[0]), pd(t, 0, 256), E1, 128 * t, W, 0, 256) for t in range(4)]
         if b == 0:
-            make_pj(1)
-            make_pj(2)
+            make_rep(1)
+            make_rep(2)
+            t_dgn = V([t_c16, t_q], vec.tensor_scalar, T.diagn[:], T.c16[:, 0:32], T.qc[:], -64.0, ALU.is_equal, ALU.mult)
         elif b == 1:
             tr_codes(2, 0, t_x1)
             tr_codes(2, 1, t_x1)
         else:
             t_wq = V([lw], vec.quantize_mx, T.wq[:], T.wqs[:], T.wt[:])
-        t_w = []
+        t_w, t_sc = [], []
         for h in range(2):
             pm = T["pm%d" % h]
             t = V([t_s[h], t_neg], vec.tensor_tensor_scan, pm[:], T.ps[:, 512 * h:512 * h + 256], T.neg[:], -1.0e29, ALU.max, ALU.max)
+            t_sc.append(t)
             t_w.append(A([t], T["sg%d" % h][:], pm[:], ACTF.Sign, bias=pm[:, 255:256], scale=-1.0, accum_out=wcb[:, h:h + 1]))
         need("G", t_w)
         g.remote_dma(wca[:], wcb[:], T.sem["rl%d" % b], T.sem.loc, pid, rid, mask)
-
-        t = V([t_w[0], t_diag], vec.tensor_scalar, T.tinb[:, 0:32], T.diag[:, 0:32], wcb[:, 0:1], None, ALU.mult)
+        if b == 0:
+            t_rs = V([t_c16], vec.tensor_scalar, T.rs[:], T.c16[:], 0.0, None, ALU.is_gt)
+        t = V([t_w[0], t_dgn], vec.tensor_scalar, T.tinb[:, 0:32], T.diagn[:], wcb[:, 0:1], None, ALU.mult)
         t_dk = [V([t_u[0]], vec.tensor_scalar, T.dk0[:], pd(0, 0, 256), 0.75, None, ALU.mult)]
         for i in (1, 2, 3):
             t_dk.append(A([t_u[i]], T["dk%d" % i][:], pd(i, 0, 256), scale=0.75))
-        t1 = V([t_w[1]], vec.tensor_scalar, T.tinb[:, 32:64], T.diag[:, 0:32], wcb[:, 1:2], None, ALU.mult)
+        t1 = V([t_w[1]], vec.tensor_scalar, T.tinb[:, 32:64], T.diagn[:], wcb[:, 1:2], None, ALU.mult)
         t = V([t, t1], vec.transpose, T.toutb[:], T.tinb[:])
         t_wr = V([t, t_rs], vec.tensor_tensor_scan, T.wrb[:], T.rs[:, 0:64], T.toutb[:], 0.0, ALU.mult, ALU.add)
-        t_wb = V([t_wr], vec.tensor_copy, wb[:], T.wrb[:, 15:64:16])
+        t_wb = V([t_wr], vec.tensor_scalar, wb[:], T.wrb[:, 15:64:16], -0.015625, None, ALU.mult)
 
         t_cs = [V([t_wb, t_dk[t], t_hs] + t_tk[b], vec.tensor_tensor, T.hs[:, t:256:4], T["dk%d" % t][:].indirect(wb[:]),
                   T["tk%d" % t][:, NT * b:NT * b + NT], ALU.add) for t in range(4)]
@@ -213,60 +208,64 @@ def rank_program(g, core, T, topo):
         g.remote_dma(w8(W[0], 256, 320), w8(W[0], 320, 384), T.sem["rd%d" % b], T.sem.loc, pid, rid, mask)
         g.remote_dma(T[W[1]][:, 256:320], T[W[1]][:, 320:384], T.sem["rd%d" % b], T.sem.loc, pid, rid, mask)
 
-        t_rb, ts = squares("eqb", "wrb", "nwb", "rb%d" % b, t_wr, t_wb)
-        t2 = A([t_diag], T.t2[:], T.diag[:].indirect(wb[:]), scale=2.0)
+        t_rb = A([t_wb, t_row], rb[:], T.row[:, 0:256].indirect(wb[:]))
+        ts = [A([t_wr], T.eqb[:, 64:260:65], T.wrb[:, 15:64:16], scale=-0.015625)]
+        ts += squares("eqb", 65, rb[:], "wrb", [t_wr, t_rb])
         if b == 0:
-            make_rows()
-            make_maps(0)
-        t3 = V([t_row], vec.tensor_tensor, T.t3[:], T.diag[:].indirect(wb[:]), T.row[:, 320:384], ALU.mult)
-        t = V(ts + [cst["mk"]], vec.tensor_tensor_scan, T.dsb[:], T.mk[:], T.eqb[:], 100000.0, ALU.add, ALU.min)
-        t_ub = V([t], vec.tensor_scalar, ub[:], T.dsb[:, 64:260:65], 64.0, None, ALU.add)
-        if b == 0:
-            t_x1 = V([lx1], vec.quantize_mx, T.xq[:, 128:256], T.xqs[:, 128:256], T.xt[:, 512:1024])
-            make_rep(1)
-            make_rep(2)
-            t_tk[1] = t_tk[2] = unpack_tokens(128, 64, 128, [t_x1] + t_dk)
-        t_mi = V([t_ub, t_maps[b], t_row], vec.tensor_copy, T.mi[:].indirect(ub[:]), T.row[:, 0:64])
-        t_ml = V([t3], vec.tensor_copy, ml[:].indirect(ub[:]), T.t3[:])
-        t_mc = V([t2], vec.tensor_copy, mc[:].indirect(ub[:]), T.t2[:])
+            t_hm = A([], T.hm[:], T.hz[:, 0:512])
+            cst["base"] = V([t_diag, t_row], vec.tensor_tensor, T.base[:], T.diag[:], T.row[:, 0:256], ALU.mult)
+            make_mk()
+            make_pj(0)
+            cst["step"] = V([t_row], vec.tensor_scalar, T.step[:], T.row[:, 0:80], 64.0, 1.0, ALU.is_lt, ALU.add)
+            t_tkm = [mx([t_x1, t_e1[i]] + t_sc, px(i, 0, 128), E1, 128 * i, XQ, 128, 128) for i in range(4)]
+            t_tk[1] = t_tk[2] = [A([t_tkm[t]], T["tk%d" % t][:, 64:192], px(t, 0, 128), scale=0.25) for t in range(4)]
+            make_ml(0)
+        arr_l = ("rl%d" % b, neng, {})
+        ta = [A([arr_l, t_dgn], T.tina[:, 32 * h:32 * h + 32], T.diagn[:], scale=wca[:, h:h + 1]) for h in range(2)]
+
+        t3 = V([t_row, t_diag], vec.tensor_tensor, T.t3[:], T.diag[:].indirect(wb[:]), T.row[:, 320:384], ALU.mult)
+        t = V(ta, vec.transpose, T.touta[:], T.tina[:])
+        t_d = V(ts + cst["mk"], vec.tensor_tensor_scan, T.dsb[:], T.mk[:], T.eqb[:], 100000.0, ALU.add, ALU.min)
+        t_wr = V([t], vec.tensor_tensor_scan, T.wra[:], T.rs[:, 0:64], T.touta[:], 0.0, ALU.mult, ALU.add)
+        tj = squares("eqj", 64, rb[:], "wra", [t_wr, t_rb])
+        t_ub = V([t_d], vec.tensor_scalar, ub[:], T.dsb[:, 64:260:65], 64.0, None, ALU.add)
+        t_wa = V([t_wr], vec.tensor_scalar, wa[:], T.wra[:, 15:64:16], -0.015625, None, ALU.mult)
+        t_ra = A([t_wa, t_row], T.ra[:], T.row[:, 0:256].indirect(wa[:]))
+        ts = [A([t_wr], T.eqa[:, 64:260:65], T.wra[:, 15:64:16], scale=-0.015625)]
+        ts += squares("eqa", 65, T.ra[:], "wra", [t_wr, t_ra])
+        t_vd = V([t_wa], vec.tensor_tensor, T.vd[:], T.diag[:].indirect(wa[:]), T.row[:, 256:320], ALU.mult)
+        t_ml = V([t3, t_ub, t_maps[b]], vec.tensor_copy, ml[:].indirect(ub[:]), T.t3[:])
+        t_j = V(tj + t_jm, vec.tensor_tensor_scan, T.dsj[:], T.jmk[:], T.eqj[:], 100000.0, ALU.add, ALU.min)
+        t_jl = V([t_j], vec.tensor_scalar, jl[:], T.dsj[:, 63:256:64], 63.0, 64.0, ALU.add, ALU.min)
+        t_p = pick(PJ, 64, 128, W, 320, 448, jl[:], [t_jl, t_pj[b]])
         if b + 1 < R:
             for h in range(2):
-                if b == 0:
-                    tr_codes(1, h, t_x1)
                 tr_scales(b + 1, h, t_x1)
-            make_maps(b + 1)
-
-        arr_l = ("rl%d" % b, neng, {})
-        ta = [A([arr_l, t_diag], T.tina[:, 32 * h:32 * h + 32], T.diag[:, 0:32], scale=wca[:, h:h + 1]) for h in range(2)]
-        t = V(ta, vec.transpose, T.touta[:], T.tina[:])
-        t_wr = V([t], vec.tensor_tensor_scan, T.wra[:], T.rs[:, 0:64], T.touta[:], 0.0, ALU.mult, ALU.add)
-        t_wa = V([t_wr], vec.tensor_copy, wa[:], T.wra[:, 15:64:16])
-        t_ra, ts = squares("eqa", "wra", "nwa", "ra", t_wr, t_wa)
-        t = V([t_wa, t_mi], vec.tensor_tensor, T.g1[:], T.mi[:, 64:320].indirect(wa[:]), T.diag[:, 0:64], ALU.mult)
-        t_va = V([t_mc], vec.tensor_tensor, T.va[:], mc[:, 64:320].indirect(wa[:]), T.row[:, 256:320], ALU.mult)
-        t = V([t], vec.tensor_tensor_scan, T.s1[:], T.rs[:, 0:64], T.g1[:], 0.0, ALU.mult, ALU.add)
-        t_jl = V([t], vec.tensor_copy, jl[:], T.s1[:, 15:64:16])
-        t_j = pick(PJ, 64, 128, W, 320, 384, jl[:], [t_jl, t_pj[b]])
-        for i in range(4):
-            mx(t_dk + t_j + t_tk[1], pd(i, 0, 128), E1, 128 * i, PJ, 0, 128, True, False)
+            make_ml(b + 1)
         arr_d = ("rd%d" % b, 2 * neng, {})
-        t_d = [mx([arr_d], pd(i, 0, 128), E1, 128 * i, W, 192, 128, False, True) for i in range(4)]
         for i in range(4):
-            t_cm = A([t_d[i], t_hm], T.hm[:, i:512:8], pd(i, 64, 128), scale=0.5)
-
+            mx([arr_d] + t_dk, pd(i, 0, 128), E1, 128 * i, W, 192, 128, True, False)
+        t_d = [mx(t_p, pd(i, 0, 128), E1, 128 * i, PJ, 0, 128, False, True) for i in range(4)]
+        t_cm = [A([t_d[i], t_hm], T.hm[:, i:512:8], pd(i, 64, 128), scale=0.5) for i in range(4)]
         t = V(ts, vec.tensor_tensor_scan, T.dsa[:], T.mk[:], T.eqa[:], 100000.0, ALU.add, ALU.min)
+        t_va = V([t_jl, t_vd, cst["step"]], vec.tensor_tensor, T.va[:], T.step[:].indirect(jl[:]), T.vd[:], ALU.mult)
         t_ua = V([t], vec.tensor_scalar, ua[:], T.dsa[:, 64:260:65], 64.0, None, ALU.add)
         t = V([t_ua, t_va, t_ml], vec.tensor_copy, ml[:].indirect(ua[:]), T.va[:])
         t = V([t], vec.tensor_tensor_scan, T.ls[:], T.rs[:], ml[:, 64:320], 0.0, ALU.mult, ALU.add)
+        if b == 0:
+            tr_codes(1, 0, t_x1)
         t_ll = V([t], vec.tensor_copy, ll[:], T.ls[:, 15:256:16])
-        t_m = V([t_cm], vec.quantize_mx, T[W[0]][:, 512:640], T[W[1]][:, 512:640], T.hm[:])
+        t_m = V(t_cm, vec.quantize_mx, T[W[0]][:, 512:640], T[W[1]][:, 512:640], T.hm[:])
         dma("S", [t_rb], "st", T.ch[b:b + 1, 0:NT], rb[0:1, :])
         if b + 1 < R:
             t_tab = pick(("win%d" % (b + 1), "wins%d" % (b + 1)), 0, 256, W, 0, 640, ll[:], [t_m, t_ll])
+            make_pj(b + 1)
+            if b == 0:
+                tr_codes(1, 1, t_x1)
 
     K = ("k3", "k3s")
     t_h = [pick(K, 128 * m, 128 * m + 128, W, 0, 640, ll[:, 8 * m:8 * m + 8], [t_m, t_ll]) for m in range(2)]
-    t_y = [mx([t_wq] + t_h[m], T.ps[:, 512 * m:512 * m + 128], ("wq", "wqs"), 0, K, 128 * m, 128, True, True) for m in range(2)]
+    t_y = [mx([t_wq] + t_h[m], T.ps[:, 512 * m:512 * m + 128], ("wq", "wqs"), 0, K, 128 * m, 128) for m in range(2)]
     t_ya = A([t_y[0]], T.yt[:, 0:128], T.ps[:, 0:128])
     dma("A", [t_ya], "st", T.y[:, 0:128], T.yt[:, 0:128])
     t_yv = V([t_y[1]], vec.tensor_copy, T.yt[:, 128:256], T.ps[:, 512:640])

from concourse.mybir import dt, AluOpType, ActivationFunctionType

ALU = AluOpType
ACTF = ActivationFunctionType
R = 3
NT = 64

X4 = "float8_e4m3fn_x4"
SCRATCH = {"ps": ("psum", [128, 1024], "float32"), "pd": ("psum", [128, 2048], "float32"), "pe": ("psum", [128, 1024], "float32"),
           "pidx": ("sbuf", [128, 1], "int32"), "pand": ("sbuf", [128, 1], "int32")}
for _n, _w in (("xt", 1024), ("kt", 1024), ("wt", 512), ("z1", 516), ("hs", 512), ("hm", 512), ("hz", 516), ("sg0", 256), ("sg1", 256)):
    SCRATCH[_n] = ("sbuf", [128, _w], "bfloat16")
for _n, _w in (("qc", 1), ("qm", 1), ("repi", 16), ("c16", 256), ("row", 384), ("iq", 260), ("mk", 260), ("diag", 256),
               ("diagn", 32), ("rs", 256), ("base", 256), ("neg", 256), ("jmk", 256), ("step", 80), ("pm0", 256), ("pm1", 256),
               ("tinb", 64), ("tina", 64), ("toutb", 64), ("touta", 64), ("wrb", 64), ("wra", 64), ("eqb", 260), ("eqa", 260),
               ("eqj", 256), ("dsb", 260), ("dsa", 260), ("dsj", 256), ("ra", 64), ("t3", 64), ("va", 64), ("vd", 64),
               ("ls", 256), ("yt", 256), ("dk0", 256), ("dk1", 256), ("dk2", 256), ("dk3", 256),
               ("tk0", 192), ("tk1", 192), ("tk2", 192), ("tk3", 192)):
    SCRATCH[_n] = ("sbuf", [128, _w], "float32")
for _n, _w in (("e1", 512), ("xq", 256), ("wq", 128), ("k3", 256)):
    SCRATCH[_n] = ("sbuf", [128, _w], X4)
    SCRATCH[_n + "s"] = ("sbuf", [128, _w], "uint8")
for _b in range(R):
    for _n, _w in (("win", 640), ("pj", 128), ("tr", 256)):
        SCRATCH["%s%d" % (_n, _b)] = ("sbuf", [128, _w], X4)
        SCRATCH["%ss%d" % (_n, _b)] = ("sbuf", [128, _w], "uint8")
    for _n, _w in (("rep", 16), ("wb", 4), ("wa", 4), ("ub", 4), ("ua", 4), ("jl", 4), ("ll", 16)):
        SCRATCH["%s%d" % (_n, _b)] = ("sbuf", [128, _w], "uint16")
    for _n, _w in (("ml", 320), ("rb", 64), ("wcb", 2), ("wca", 2)):
        SCRATCH["%s%d" % (_n, _b)] = ("sbuf", [128, _w], "float32")

SEMAPHORES = ["cv", "ca", "cp", "cg", "lx0", "lx1", "lk", "lw", "st", "loc"]
for _b in range(R):
    SEMAPHORES += ["rl%d" % _b, "rd%d" % _b]


def rank_program(g, core, T, topo):
    rank = T.rank_of(core)
    if rank is None:
        return
    queues = {"V": (g.vector, "cv"), "A": (g.scalar, "ca"), "P": (g.tensor, "cp"), "G": (g, "cg"), "S": (g.sync, None)}
    issued = {"cv": 0, "ca": 0, "cp": 0, "cg": 0}
    known = {q: {} for q in queues}

    def need(q, deps):
        for sem, val, through in deps:
            if known[q].get(sem, 0) < val:
                queues[q][0].wait_ge(T.sem[sem], val)
                known[q][sem] = val
                for s, v in through.items():
                    known[q][s] = max(known[q].get(s, 0), v)

    def do(q, deps, fn, *args, **kw):
        need(q, deps)
        sem = queues[q][1]
        issued[sem] += 1
        fn(*args, **kw).then_inc(T.sem[sem], 1)
        return (sem, issued[sem], dict(known[q]))

    def dma(q, deps, sem, out, in_):
        need(q, deps)
        queues[q][0].dma_start(out, in_).then_inc(T.sem[sem], 16)
        return (sem, 16, dict(known[q]))

    vec, act, ten = g.vector, g.scalar, g.tensor

    def V(deps, fn, *args, **kw):
        return do("V", deps, fn, *args, **kw)

    def A(deps, out, in_, func=ACTF.Copy, **kw):
        return do("A", deps, act.activation, out, in_, func, **kw)

    def mx(deps, bank, st, a, mv, c, n, start=True, stop=True):
        return do("P", deps, ten.matmul_mx, bank, T[st[0]][:, a:a + 128], T[st[1]][:, a:a + 128],
                  T[mv[0]][:, c:c + n], T[mv[1]][:, c:c + n], start, stop)

    def pd(t, a, b):
        return T.pd[:, 512 * t + a:512 * t + b]

    def px(t, a, b):
        return (T.ps, T.pe)[t // 2][:, 512 * (t % 2) + a:512 * (t % 2) + b]

    def w8(name, a, b):
        return T[name][:, a:b].bitcast(dt.uint8)

    def w32(name, a, b):
        return T[name][:, a:b].bitcast(dt.uint32)

    def pick(out, a, b, win, c, d, off, deps):
        tc = V(deps, vec.tensor_copy, w32(out[0], a, b), w32(win[0], c, d).indirect(off))
        ts = A(deps, T[out[1]][:, a:b], T[win[1]][:, c:d].indirect(off))
        return [tc, ts]

    E1, XQ = ("e1", "e1s"), ("xq", "xqs")

    lx0 = dma("S", [], "lx0", T.xt[:, 0:256], T.x[:, 0:256])
    lk = dma("A", [], "lk", T.kt[:], T.kb[:])
    lx1 = dma("S", [], "lx1", T.xt[:, 512:1024], T.x[:, 256:768])
    lw = dma("S", [], "lw", T.wt[:], T.w[:])

    t_z0 = V([], vec.memset, T.z1[:], 0.0)
    t_pidx = do("G", [], g.iota, T.pidx[:], [[0, 1]], 0, 1)
    t_repi = do("G", [], g.iota, T.repi[:], [[32, 2], [0, 4], [16, 2]], 0, 0, allow_small_or_imprecise_dtypes=True)
    t_z1 = do("G", [t_z0], g.affine_select, T.z1[:, 3:515:4], T.z1[:, 3:515:4], [[-1, 128]], ALU.not_equal, 1.0, 0, 1)
    t_c16 = do("G", [], g.iota, T.c16[:], [[0, 16], [1, 16]], 0, 0, allow_small_or_imprecise_dtypes=True)
    t_row = do("G", [], g.iota, T.row[:], [[1, 384]], 0, 0, allow_small_or_imprecise_dtypes=True)
    t_iq = do("G", [], g.iota, T.iq[:], [[-16, 4], [1, 65]], 0, 0, allow_small_or_imprecise_dtypes=True)

    t_hz = V([], vec.memset, T.hz[:], 0.0)
    t_xz = A([t_hz], T.xt[:, 256:512], T.hz[:, 0:256])
    t_and = V([t_pidx], vec.tensor_scalar, T.pand[:], T.pidx[:], 15, None, ALU.bitwise_and)
    t_q = V([t_and], vec.tensor_copy, T.qc[:], T.pand[:])
    t_neg = A([t_hz], T.neg[:], T.hz[:, 0:256], ACTF.Copy, bias=-1.0e29)
    t_jm = [A([t_hz], T.jmk[:], T.hz[:, 0:256], ACTF.Copy, bias=-1.0)]
    t_jm.append(A(t_jm, T.jmk[:, 0:256:64], T.hz[:, 0:4], ACTF.Copy, bias=100000.0))
    t_rep, t_pj, t_e1 = {}, {}, []

    def make_rep(b):
        t_rep[b] = V([t_q, t_repi], vec.tensor_scalar, T["rep%d" % b][:], T.repi[:], T.qc[:], float((0, 128, 192)[b]), ALU.add, ALU.add)

    def make_pj(b):
        t_pj[b] = V([t_hz], vec.quantize_mx, T["pj%d" % b][:], T["pjs%d" % b][:], T.hz[:, 0:512])

    t_tr = [[] for _ in range(2 * R)]
    t_tk = {}

    def tr_codes(b, h, dep):
        t_tr[2 * b + h].append(V([dep, t_rep[b]], vec.tensor_copy, w32("tr%d" % b, 128 * h, 128 * h + 128),
                                 w32("xq", 0, 256 if b else 128).indirect(T["rep%d" % b][:, 8 * h:8 * h + 8])))

    def tr_scales(b, h, dep):
        t_tr[2 * b + h].append(A([dep, t_rep[b]], T["trs%d" % b][:, 128 * h:128 * h + 128],
                                 T.xqs[:, 0:256 if b else 128].indirect(T["rep%d" % b][:, 8 * h:8 * h + 8])))

    make_rep(0)
    t_x0 = V([lx0, t_xz], vec.quantize_mx, T.xq[:, 0:128], T.xqs[:, 0:128], T.xt[:, 0:512])
    for i in range(4):
        t_e1.append(V([t_z1], vec.quantize_mx, T.e1[:, 128 * i:128 * i + 128], T.e1s[:, 128 * i:128 * i + 128], T.z1[:, 3 - i:515 - i]))
    tr_codes(0, 0, t_x0)
    for h in range(2):
        tr_scales(0, h, t_x0)
    t_tab = [V([lk], vec.quantize_mx, T.win0[:, 0:256], T.wins0[:, 0:256], T.kt[:])]
    tr_codes(0, 1, t_x0)
    t_tkm = [mx([t_x0, t_e1[t]], pd(t, 0, 128), E1, 128 * t, XQ, 0, 128) for t in range(4)]
    t_tk[0] = [A([t_tkm[t]], T["tk%d" % t][:, 0:64], pd(t, 0, 64), scale=0.25) for t in range(4)]
    t_hs = A([], T.hs[:], T.hz[:, 0:512])
    t_diag = V([t_c16, t_q], vec.tensor_scalar, T.diag[:], T.c16[:], T.qc[:], None, ALU.is_equal)
    t_x1 = V([lx1], vec.quantize_mx, T.xq[:, 128:256], T.xqs[:, 128:256], T.xt[:, 512:1024])
    cst, t_maps = {}, {}

    def make_mk():
        t_m = V([t_iq], vec.tensor_scalar, T.mk[:], T.iq[:], T.qc[:], -2000.0, ALU.is_equal, ALU.mult)
        t_qm = V([t_q], vec.tensor_scalar, T.qm[:], T.qc[:], 2000.0, None, ALU.add)
        t_m1 = V([t_m], vec.tensor_scalar, T.mk[:, 65:260:65], T.iq[:, 65:260:65], 0.0, 100000.0, ALU.mult, ALU.add)
        t_m = V([t_m, t_qm], vec.tensor_scalar, T.mk[:, 64:260:65], T.iq[:, 64:260:65], -1.0, T.qm[:], ALU.mult, ALU.add)
        cst["mk"] = [t_m1, t_m]

    def make_ml(b):
        t_maps[b] = A([cst["base"]], T["ml%d" % b][:, 64:320], T.base[:])

    def squares(eq, n, row, wr, deps):
        return [A(deps, T[eq][:, n * k:n * k + 64], row, ACTF.Square, bias=T[wr][:, 16 * k + 15:16 * k + 16], scale=64.0)
                for k in range(4)]

    for b in range(R):
        W, PJ, TR = ("win%d" % b, "wins%d" % b), ("pj%d" % b, "pjs%d" % b), ("tr%d" % b, "trs%d" % b)
        wb, wa, ub, ua, jl, ll = [T["%s%d" % (n, b)] for n in ("wb", "wa", "ub", "ua", "jl", "ll")]
        ml, rb, wcb, wca = [T["%s%d" % (n, b)] for n in ("ml", "rb", "wcb", "wca")]
        dst = T.cores[rank ^ (1 << b)]
        rid, pid, _s = topo.addr(dst)
        mask = topo.mask(core, dst)
        neng = len(topo.engines(core, dst))

        t_s = [mx(t_tab + t_tr[2 * b + h], T.ps[:, 512 * h:512 * h + 256], TR, 128 * h, W, 0, 256) for h in range(2)]
        t_u = [mx([t_e1[t]] + (t_cm if b else t_tk[0]), pd(t, 0, 256), E1, 128 * t, W, 0, 256) for t in range(4)]
        if b == 0:
            make_rep(1)
            make_rep(2)
            t_dgn = V([t_c16, t_q], vec.tensor_scalar, T.diagn[:], T.c16[:, 0:32], T.qc[:], -64.0, ALU.is_equal, ALU.mult)
        elif b == 1:
            tr_codes(2, 0, t_x1)
            tr_codes(2, 1, t_x1)
        else:
            t_wq = V([lw], vec.quantize_mx, T.wq[:], T.wqs[:], T.wt[:])
        t_w, t_sc = [], []
        for h in range(2):
            pm = T["pm%d" % h]
            t = V([t_s[h], t_neg], vec.tensor_tensor_scan, pm[:], T.ps[:, 512 * h:512 * h + 256], T.neg[:], -1.0e29, ALU.max, ALU.max)
            t_sc.append(t)
            t_w.append(A([t], T["sg%d" % h][:], pm[:], ACTF.Sign, bias=pm[:, 255:256], scale=-1.0, accum_out=wcb[:, h:h + 1]))
        need("G", t_w)
        g.remote_dma(wca[:], wcb[:], T.sem["rl%d" % b], T.sem.loc, pid, rid, mask)
        if b == 0:
            t_rs = V([t_c16], vec.tensor_scalar, T.rs[:], T.c16[:], 0.0, None, ALU.is_gt)
        t = V([t_w[0], t_dgn], vec.tensor_scalar, T.tinb[:, 0:32], T.diagn[:], wcb[:, 0:1], None, ALU.mult)
        t_dk = [V([t_u[0]], vec.tensor_scalar, T.dk0[:], pd(0, 0, 256), 0.75, None, ALU.mult)]
        for i in (1, 2, 3):
            t_dk.append(A([t_u[i]], T["dk%d" % i][:], pd(i, 0, 256), scale=0.75))
        t1 = V([t_w[1]], vec.tensor_scalar, T.tinb[:, 32:64], T.diagn[:], wcb[:, 1:2], None, ALU.mult)
        t = V([t, t1], vec.transpose, T.toutb[:], T.tinb[:])
        t_wr = V([t, t_rs], vec.tensor_tensor_scan, T.wrb[:], T.rs[:, 0:64], T.toutb[:], 0.0, ALU.mult, ALU.add)
        t_wb = V([t_wr], vec.tensor_scalar, wb[:], T.wrb[:, 15:64:16], -0.015625, None, ALU.mult)

        t_cs = [V([t_wb, t_dk[t], t_hs] + t_tk[b], vec.tensor_tensor, T.hs[:, t:256:4], T["dk%d" % t][:].indirect(wb[:]),
                  T["tk%d" % t][:, NT * b:NT * b + NT], ALU.add) for t in range(4)]
        t_n = V(t_cs, vec.quantize_mx, T[W[0]][:, 320:448], T[W[1]][:, 320:448], T.hs[:])
        need("G", [t_n])
        g.remote_dma(w8(W[0], 256, 320), w8(W[0], 320, 384), T.sem["rd%d" % b], T.sem.loc, pid, rid, mask)
        g.remote_dma(T[W[1]][:, 256:320], T[W[1]][:, 320:384], T.sem["rd%d" % b], T.sem.loc, pid, rid, mask)

        t_rb = A([t_wb, t_row], rb[:], T.row[:, 0:256].indirect(wb[:]))
        ts = [A([t_wr], T.eqb[:, 64:260:65], T.wrb[:, 15:64:16], scale=-0.015625)]
        ts += squares("eqb", 65, rb[:], "wrb", [t_wr, t_rb])
        if b == 0:
            t_hm = A([], T.hm[:], T.hz[:, 0:512])
            cst["base"] = V([t_diag, t_row], vec.tensor_tensor, T.base[:], T.diag[:], T.row[:, 0:256], ALU.mult)
            make_mk()
            make_pj(0)
            cst["step"] = V([t_row], vec.tensor_scalar, T.step[:], T.row[:, 0:80], 64.0, 1.0, ALU.is_lt, ALU.add)
            t_tkm = [mx([t_x1, t_e1[i]] + t_sc, px(i, 0, 128), E1, 128 * i, XQ, 128, 128) for i in range(4)]
            t_tk[1] = t_tk[2] = [A([t_tkm[t]], T["tk%d" % t][:, 64:192], px(t, 0, 128), scale=0.25) for t in range(4)]
            make_ml(0)
        arr_l = ("rl%d" % b, neng, {})
        ta = [A([arr_l, t_dgn], T.tina[:, 32 * h:32 * h + 32], T.diagn[:], scale=wca[:, h:h + 1]) for h in range(2)]

        t3 = V([t_row, t_diag], vec.tensor_tensor, T.t3[:], T.diag[:].indirect(wb[:]), T.row[:, 320:384], ALU.mult)
        t = V(ta, vec.transpose, T.touta[:], T.tina[:])
        t_d = V(ts + cst["mk"], vec.tensor_tensor_scan, T.dsb[:], T.mk[:], T.eqb[:], 100000.0, ALU.add, ALU.min)
        t_wr = V([t], vec.tensor_tensor_scan, T.wra[:], T.rs[:, 0:64], T.touta[:], 0.0, ALU.mult, ALU.add)
        tj = squares("eqj", 64, rb[:], "wra", [t_wr, t_rb])
        t_ub = V([t_d], vec.tensor_scalar, ub[:], T.dsb[:, 64:260:65], 64.0, None, ALU.add)
        t_wa = V([t_wr], vec.tensor_scalar, wa[:], T.wra[:, 15:64:16], -0.015625, None, ALU.mult)
        t_ra = A([t_wa, t_row], T.ra[:], T.row[:, 0:256].indirect(wa[:]))
        ts = [A([t_wr], T.eqa[:, 64:260:65], T.wra[:, 15:64:16], scale=-0.015625)]
        ts += squares("eqa", 65, T.ra[:], "wra", [t_wr, t_ra])
        t_vd = V([t_wa], vec.tensor_tensor, T.vd[:], T.diag[:].indirect(wa[:]), T.row[:, 256:320], ALU.mult)
        t_ml = V([t3, t_ub, t_maps[b]], vec.tensor_copy, ml[:].indirect(ub[:]), T.t3[:])
        t_j = V(tj + t_jm, vec.tensor_tensor_scan, T.dsj[:], T.jmk[:], T.eqj[:], 100000.0, ALU.add, ALU.min)
        t_jl = V([t_j], vec.tensor_scalar, jl[:], T.dsj[:, 63:256:64], 63.0, 64.0, ALU.add, ALU.min)
        t_p = pick(PJ, 64, 128, W, 320, 448, jl[:], [t_jl, t_pj[b]])
        if b + 1 < R:
            for h in range(2):
                tr_scales(b + 1, h, t_x1)
            make_ml(b + 1)
        arr_d = ("rd%d" % b, 2 * neng, {})
        for i in range(4):
            mx([arr_d] + t_dk, pd(i, 0, 128), E1, 128 * i, W, 192, 128, True, False)
        t_d = [mx(t_p, pd(i, 0, 128), E1, 128 * i, PJ, 0, 128, False, True) for i in range(4)]
        t_cm = [A([t_d[i], t_hm], T.hm[:, i:512:8], pd(i, 64, 128), scale=0.5) for i in range(4)]
        t = V(ts, vec.tensor_tensor_scan, T.dsa[:], T.mk[:], T.eqa[:], 100000.0, ALU.add, ALU.min)
        t_va = V([t_jl, t_vd, cst["step"]], vec.tensor_tensor, T.va[:], T.step[:].indirect(jl[:]), T.vd[:], ALU.mult)
        t_ua = V([t], vec.tensor_scalar, ua[:], T.dsa[:, 64:260:65], 64.0, None, ALU.add)
        t = V([t_ua, t_va, t_ml], vec.tensor_copy, ml[:].indirect(ua[:]), T.va[:])
        t = V([t], vec.tensor_tensor_scan, T.ls[:], T.rs[:], ml[:, 64:320], 0.0, ALU.mult, ALU.add)
        if b == 0:
            tr_codes(1, 0, t_x1)
        t_ll = V([t], vec.tensor_copy, ll[:], T.ls[:, 15:256:16])
        t_m = V(t_cm, vec.quantize_mx, T[W[0]][:, 512:640], T[W[1]][:, 512:640], T.hm[:])
        dma("S", [t_rb], "st", T.ch[b:b + 1, 0:NT], rb[0:1, :])
        if b + 1 < R:
            t_tab = pick(("win%d" % (b + 1), "wins%d" % (b + 1)), 0, 256, W, 0, 640, ll[:], [t_m, t_ll])
            make_pj(b + 1)
            if b == 0:
                tr_codes(1, 1, t_x1)

    K = ("k3", "k3s")
    t_h = [pick(K, 128 * m, 128 * m + 128, W, 0, 640, ll[:, 8 * m:8 * m + 8], [t_m, t_ll]) for m in range(2)]
    t_y = [mx([t_wq] + t_h[m], T.ps[:, 512 * m:512 * m + 128], ("wq", "wqs"), 0, K, 128 * m, 128) for m in range(2)]
    t_ya = A([t_y[0]], T.yt[:, 0:128], T.ps[:, 0:128])
    dma("A", [t_ya], "st", T.y[:, 0:128], T.yt[:, 0:128])
    t_yv = V([t_y[1]], vec.tensor_copy, T.yt[:, 128:256], T.ps[:, 512:640])
    for m in range(2):
        dma("S", t_h[m][0:1], "st", T.oc[:, 512 * m:512 * m + 512], w8("k3", 128 * m, 128 * m + 128))
    for k in range(4):
        dma("AASS"[k], t_h[1][1:2], "st", T.osc[4 * k:4 * k + 4, :], T.k3s[32 * k:32 * k + 4, :])
    dma("S", [t_yv], "st", T.y[:, 128:256], T.yt[:, 128:256])
    g.sync.wait_ge(T.sem.st, 16 * (R + 8))
    g.wait_ge(T.sem.loc, 3 * R * neng)
